import numpy as np, ml_dtypes
CORES = [9,25,41,57]
N = 4
BF = ml_dtypes.bfloat16
C, S, M, B, LB, A, CL = 8, 2560, 16, 64, 6, 20, 255
def fold(p):
    p = np.asarray(p, np.int64)[..., None, None]; n = np.arange(M)[:, None]; b = np.arange(B)[None, :]
    return ((n * p + b * (p >> LB)) >> 8).reshape(p.shape[:-2] + (M * B,))
def bend(t, a):
    return t + ((a * (t >> 3) ** 2) >> 12)
def trials(rng, a, h):
    v = bend(np.arange(S, dtype=np.int64), a[..., None]); last = np.sum(np.maximum.accumulate(v, -1) < S, -1) - 1
    p = np.maximum(256 * (last + 1) * h // (64 * M), 256); room = last - fold(p)[..., -1]
    return p, rng.integers(0, room[..., None] + 1, (N, 8, N * C)), room
def given(x, p, a, de):
    return {"x": x.reshape(N, 16, C * S).astype(np.float32).astype(BF), "pa": np.stack([p, a], -1).astype(np.int32), "de": de.astype(np.int32)}
def setup_inputs(rng):
    a = rng.integers(-A, A + 1, (N, 8)); p, de, room = trials(rng, a, rng.integers(32, 58, (N, 8)))
    return given(rng.integers(0, 16, (N, 16, C, S)), p, a, de)
def setup_inputs_ends(rng):
    a = rng.permuted(np.tile(np.array([-A, -A, -1, 0, 0, 1, A, A]), (N, 1)), axis=1)
    h = rng.permuted(np.tile(np.array([0, 0, 20, 40, 40, 60, 64, 64]), (N, 1)), axis=1)
    p, de, room = trials(rng, a, h); far = rng.permuted(np.tile(np.arange(N * C) % 2, (N, 8, 1)), axis=2)
    return given(rng.integers(0, 16, (N, 16, C, S)), p, a, far * room[..., None])
def setup_inputs_brink(rng):
    a = rng.integers(-A, A + 1, (N, 8)); p, de, room = trials(rng, a, rng.integers(32, 58, (N, 8)))
    u = rng.integers(0, 8, (N, 16, C, S)); return given(8 + (u == 0) - 1 * (u == 1), p, a, de)
def setup_inputs_alike(rng):
    a = np.repeat(rng.integers(-A, A + 1, (N, 1)), 8, axis=1); p, de, room = trials(rng, a, np.repeat(rng.integers(16, 61, (N, 1)), 8, axis=1))
    q = rng.integers(0, N); de[q] = de[q, :1]; return given(rng.integers(0, 16, (N, 16, C, S)), p, a, de)
def setup_inputs_spread(rng):
    a = rng.integers(-A, A + 1, (N, 8)); p, de, room = trials(rng, a, rng.integers(1, 65, (N, 8)))
    v = rng.integers(0, 16, (N, 16, C, S)); m = rng.integers(0, 16, (N, 16, C, 1)); up = rng.permutation(np.arange(16) % 2).reshape(1, 16, 1, 1)
    v = np.where(up == 1, np.maximum(v, m), np.minimum(v, m)); k = rng.permutation(16)[:3]; v[:, k[:2]] = 15; v[:, k[2]] = 0
    return given(v, p, a, de)
def check_inputs(d):
    try:
        bad = []; x = np.asarray(d["x"]).astype(np.float32); pa = np.asarray(d["pa"]).astype(np.int64); de = np.asarray(d["de"]).astype(np.int64)
        if x.shape != (N, 16, C * S) or pa.shape != (N, 8, 2) or de.shape != (N, 8, N * C): return ["shapes"]
        if not (np.isfinite(x).all() and (x == np.floor(x)).all() and x.min() >= 0 and x.max() <= 15): bad.append("samples")
        if pa[..., 0].min() < 256: bad.append("periods")
        if np.abs(pa[..., 1]).max() > A: bad.append("accelerations")
        if de.min() < 0: bad.append("delays")
        t = fold(pa[..., 0])[:, :, None, :] + de[..., None]
        if t.min() < 0 or t.max() >= S: bad.append("times")
        s = bend(t, pa[..., 1][:, :, None, None])
        if s.min() < 0 or s.max() >= S: bad.append("places")
        return bad
    except Exception:
        return ["form"]
def reference(x, pa, de):
    v = x.astype(np.float32).astype(np.int64).reshape(N, 16, C, S); y = np.zeros((N, 8, 16, B), np.int64)
    for r in range(N):
        for g in range(8):
            fp = fold(pa[r, g, 0]); a = int(pa[r, g, 1]); tot = np.zeros((16, M * B), np.int64)
            for q in range(N):
                for c in range(C):
                    tot += v[q, :, c][:, bend(fp + int(de[r, g, C * q + c]), a)]
            y[r, g] = np.add.reduce(np.minimum(tot, CL).reshape(16, M, B), axis=1)
    return {"y": y.reshape(N, 128, B).astype(np.float32)}

@@ -1,0 +1,375 @@
+from concourse.bass import DstId, RemoteDMATransfer
+from concourse.mybir import AluOpType, ActivationFunctionType
+
+NS = 2560
+HALF = NS // 2
+CENTER = 1280
+BIG8 = 1.5 * 2.0 ** 26
+BIG1 = 2.0 ** 23
+LIFT = 1536
+KROWS = 105
+
+SCRATCH = {}
+for _dt, _bufs in (
+        ("int32", dict(raw=4, qi=4, tab=512, t16=16, t16b=16)),
+        ("float32", dict(par=4, msg1=4, msg2=4, ag=4, mask=128, sq=2048, ysb=64)),
+        ("float16", dict(rhs=512, lm=384, big=128, idh=128, shm=2048)),
+        ("uint16", dict(off=2048)),
+        ("bfloat16", dict(sel=16, cb=192, nfold=64, zb=128, xw=NS, xn=NS, xh=HALF, gb0=8192, gb1=8192, gb2=8192,
+                          gb3=8192, out1=1024, out2=1024, land1=1024, land2=1024, clip=1024))):
+    for _k, _w in _bufs.items():
+        SCRATCH[_k] = ("sbuf", [128, _w], _dt)
+for _k in ("pu", "pt", "pr0", "pr1", "po0", "po1", "po2", "py"):
+    SCRATCH[_k] = ("psum", [128, 512], "float32")
+SEMAPHORES = ["sv", "ss", "sp", "sg", "ld", "ldx", "st", "sent", "m1", "m2", "xa", "hx",
+              "l1a", "l1b", "l2a", "l2b"]
+
+JOBS = {"0a": (0, 0, 128, "pu", "pt"), "0b": (0, 128, 512, "pr0", "pr1"), "3": (3, 0, 512, "pu", "pt"),
+        "1a": (1, 0, 128, "pr0", "pr1"), "1b": (1, 128, 512, "pu", "pt"), "2": (2, 0, 512, "pu", "pt")}
+
+V_ORDER = [
+    ("sh", "0a"), ("pre2",), ("conv", "0a"), ("sh", "0b"), ("pre3",), ("conv", "0b"),
+    ("g", 0, 120, 176), ("lm", 3), ("g", 0, 224, 320), ("sh", "3"), ("g", 0, 376, 400), ("conv", "3"),
+    ("lm", 1), ("g", 0, 456, 488), ("sh", "1a"), ("conv", "1a"), ("sh", "1b"), ("g", 1, 96, 112), ("conv", "1b"),
+    ("g", 1, 112, 160), ("lm", 2), ("g", 1, 224, 320), ("sh", "2"), ("g", 1, 376, 416), ("conv", "2"),
+    ("g", 1, 456, 512),
+    ("g", 2, 80, 144), ("g", 2, 208, 280), ("g", 2, 336, 400), ("g", 2, 456, 512),
+    ("g", 3, 48, 128), ("g", 3, 200, 280), ("g", 3, 352, 448), ("g", 3, 448, 480),
+    ("clip", 2), ("end",),
+]
+S_ORDER = [
+    ("sq", "0a"), ("sq", "0b"), ("g", 0, 0, 120), ("g", 0, 176, 224), ("sq", "3"), ("g", 0, 320, 376),
+    ("g", 0, 400, 456), ("sq", "1a"), ("sq", "1b"), ("g", 0, 488, 512),
+    ("g", 1, 0, 96), ("g", 1, 160, 224), ("sq", "2"), ("g", 1, 320, 376), ("ev", 1, 0), ("g", 1, 416, 456),
+    ("g", 2, 0, 80), ("ev", 1, 1), ("g", 2, 144, 208), ("g", 2, 280, 336), ("ev", 2, 0), ("g", 2, 400, 456),
+    ("g", 3, 0, 48), ("ev", 2, 1), ("g", 3, 128, 200), ("g", 3, 280, 352), ("clip", 0), ("g", 3, 480, 512),
+    ("clip", 1),
+]
+
+
+def pairs(b, lo, hi):
+    return [("r", b, m) for m in range(lo, hi)]
+
+
+P_ORDER = (
+    [("u", "0a"), ("a", 0), ("u", "0b"), ("t", "0a"), ("add", "0a"), ("t", "0b"), ("add", "0b"),
+     ("u", "3"), ("t", "3"), ("open",)] + pairs(0, 0, 3) + [("add", "3")] + pairs(0, 3, 5)
+    + [("u", "1a"), ("a", 1), ("u", "1b"), ("t", "1a"), ("add", "1a"), ("t", "1b"), ("add", "1b")]
+    + pairs(0, 5, 8) + pairs(1, 0, 2) + [("u", "2"), ("a", 2), ("t", "2")] + pairs(1, 2, 4) + [("add", "2")]
+    + pairs(1, 4, 8) + pairs(2, 0, 8)
+    + [("land", 1, 0), ("land", 1, 1), ("land", 1, 2)] + pairs(3, 0, 4) + [("land", 2, 0)] + pairs(3, 4, 7)
+    + [("land", 2, 1), ("land", 2, 2), ("sum", 0), ("r", 3, 7), ("sum", 2), ("sum", 1)]
+)
+OWN = [("po0", 0, 4), ("po1", 4, 7), ("po2", 7, 8)]
+
+
+def bits(engines):
+    return sum(1 << e for e in engines)
+
+
+def helper_of(core, T, topo, dst):
+    for c in topo.cores_of(core):
+        if topo.die(c) != topo.die(core) and T.rank_of(c) is None and topo.may_write(c, dst):
+            return c
+    return None
+
+
+def rank_program(g, core, T, topo):
+    cores = list(T.cores)
+    n = len(cores)
+    rank = T.rank_of(core)
+    sem = T.sem
+    if rank is None:
+        for r in range(n):
+            dst = cores[(r - 1) % n]
+            if helper_of(cores[r], T, topo, dst) == core:
+                far = topo.engines(cores[r], dst)
+                near = [e for e in topo.engines(cores[r], core) if e not in far]
+                mine = topo.engines(core, dst)
+                rid, pid, _ = topo.addr(dst)
+                g.wait_ge(sem.hx, len(near))
+                g.remote_dma(T.xn[:, HALF:NS], T.xh[:], sem.xa, sem.sent, pid, rid, bits(mine))
+                g.wait_ge(sem.sent, len(mine))
+        return
+
+    A = AluOpType
+    F = ActivationFunctionType
+    q = rank
+    queues = {"v": g.vector, "s": g.scalar, "p": g.tensor, "g": g, "y": g.sync}
+    counts = {"sv": 0, "ss": 0, "sp": 0, "sg": 0}
+    own_sem = {"v": "sv", "s": "ss", "p": "sp", "g": "sg"}
+    seen = {}
+    done = {}
+
+    def wait(qn, deps):
+        need = {}
+        for d in deps:
+            s, c = done[d] if d in done else d
+            need[s] = max(need.get(s, 0), c)
+        for s, c in need.items():
+            if seen.get((qn, s), 0) < c:
+                queues[qn].wait_ge(sem[s], c)
+                seen[(qn, s)] = c
+
+    def mark(qn, ins, key):
+        s = own_sem[qn]
+        ins.then_inc(sem[s], 1)
+        counts[s] += 1
+        assert done[key] == (s, counts[s]), key
+
+    def far_engines(src, dst):
+        return topo.engines(cores[src % n], cores[dst % n])
+
+    h_in = helper_of(cores[(q + 1) % n], T, topo, core)
+    arr = {"m1": q + 1, "m2": q + 2, "l1a": q - 1, "l1b": q - 1, "l2a": q - 2, "l2b": q - 2}
+    arr = {k: (k, len(far_engines(r, q))) for k, r in arr.items()}
+    arr["xa"] = ("xa", len(far_engines(q + 1, q)) + len(topo.engines(h_in, core)))
+    LD, LDX = ("ld", 7 * 16), ("ldx", 8 * 16)
+
+    v_keys = ["mask1", "cb1", "qi1", "ag0", "ag1", "ag2", "ag3", "par0", "ag4", "ag5", "ag6", "ag7",
+              "tabn", "big", "rhs", "qa", "qb", "pd", "pq", ("lm", 0), "pa", "pq2", "idh"]
+    for o in V_ORDER:
+        v_keys += {"pre2": ["nfold1", "zb"], "pre3": ["t16b", "sel"]}.get(o[0], [o])
+    g_keys = ["tab", "maskd", "maskq", "maskp", "idb", "t16", "f0", "f1", "nf0", "nf1"]
+    for name, keys in (("sv", v_keys), ("ss", S_ORDER), ("sp", P_ORDER), ("sg", g_keys)):
+        for i, k in enumerate(keys):
+            done[k] = (name, i + 1)
+
+    def gathers(b, lo, hi):
+        return [o for o in V_ORDER + S_ORDER if o[0] == "g" and o[1] == b and o[2] < hi and o[3] > lo]
+
+    def job_of(b, lo, hi):
+        return [j for j, w in JOBS.items() if w[0] == b and w[1] < hi and w[2] > lo]
+
+    for qn, ds, rows, chans in (("y", (0, 1), (64, 72), range(0, 4)), ("s", (2, 3), (96,), range(4, 8))):
+        e = queues[qn]
+        for r0 in rows:
+            e.dma_start(T.raw[r0:r0 + 8, 0:2], T.pa[:, :]).then_inc(sem.ld, 16)
+        for j in ds:
+            d = (q + j) % n
+            e.dma_start(T.raw[0:64, j:j + 1], T.de[:, 8 * d:8 * d + 8]).then_inc(sem.ld, 16)
+        for c in chans:
+            e.dma_start(T.xw[16 * c:16 * c + 16, :], T.x[:, NS * c:NS * (c + 1)]).then_inc(sem.ldx, 16)
+
+    sent = [0]
+
+    def send(out_ap, in_ap, name, to):
+        eng = far_engines(q, to)
+        rid, pid, _ = topo.addr(cores[to % n])
+        g.remote_dma(out_ap, in_ap, sem[name], sem.sent, pid, rid, bits(eng))
+        sent[0] += len(eng)
+
+    def gop(key, deps, make):
+        wait("g", deps + [("sg", counts["sg"])])
+        mark("g", make(), key)
+
+    def pick(key, deps, view, pat):
+        gop(key, deps, lambda: g.affine_select(view, view, pat, A.is_equal, 0.0, 0, 1))
+
+    gop("tab", [], lambda: g.iota(T.tab[:], [[1, 512]], 0, 0))
+    pick("maskd", ["mask1"], T.mask[0:64, :], [[-1, 8], [0, 2], [-8, 8]])
+    pick("maskq", [], T.mask[64:96, :], [[0, 8], [-8, 2], [-1, 8]])
+    pick("maskp", [], T.mask[96:104, :], [[0, 16], [-1, 8]])
+    pick("idb", ["cb1"], T.cb[:, 0:128], [[-1, 128]])
+    gop("t16", [], lambda: g.iota(T.t16[:], [[-1, 16]], 16, 1))
+    wait("g", ["pq2"])
+    send(T.msg1[:], T.par[:], "m1", q - 1)
+    send(T.msg2[:], T.par[:], "m2", q + 2)
+    to = cores[(q - 1) % n]
+    h_out = helper_of(core, T, topo, to)
+    far = topo.engines(core, to)
+    near = [e for e in topo.engines(core, h_out) if e not in far]
+    rid, pid, _ = topo.addr(to)
+    hrid, hpid, _ = topo.addr(h_out)
+    wait("g", [LDX])
+    g.remote_dma_fused([
+        RemoteDMATransfer(dst_ids=[DstId(rid=rid, pnc=pid)], dma_engine_mask=bits(far), remote_sem=sem.xa,
+                          src=T.xw[:, 0:HALF], dst=T.xn[:, 0:HALF]),
+        RemoteDMATransfer(dst_ids=[DstId(rid=hrid, pnc=hpid)], dma_engine_mask=bits(near), remote_sem=sem.hx,
+                          src=T.xw[:, HALF:NS], dst=T.xh[:]),
+    ], local_sem=sem.sent)
+    sent[0] += len(far) + len(near)
+    for key, view in (("f0", T.cb[0:64, 128:192]), ("f1", T.cb[64:128, 128:192]),
+                      ("nf0", T.nfold[0:64, :]), ("nf1", T.nfold[64:128, :])):
+        pick(key, ["nfold1"], view, [[-1, 64]])
+    for o in S_ORDER:
+        if o[0] == "ev":
+            b, k = o[1], o[2]
+            wait("g", [o])
+            send(T["land%d" % b][:, 512 * k:512 * k + 512], T["out%d" % b][:, 512 * k:512 * k + 512],
+                 "l%d%s" % (b, "ab"[k]), q + b)
+
+    v = g.vector
+
+    def vop(key, deps, make):
+        wait("v", deps)
+        mark("v", make(), key)
+
+    for key, view, val in (
+            ("mask1", T.mask[:], 1.0), ("cb1", T.cb[:], 1.0), ("qi1", T.qi[64:128, :], 1),
+            ("ag0", T.ag[:, 0:1], 0.0), ("ag1", T.ag[0:64, 1:2], 2048.0), ("ag2", T.ag[64:96, 1:2], 1.0 / 256),
+            ("ag3", T.ag[96:128, 1:2], -2047.0 / 512), ("par0", T.par[64:128, :], 0.0),
+            ("ag4", T.ag[64:80, 0:1], 2.0 / 256), ("ag5", T.ag[96:104, 0:1], 1.0 / 256),
+            ("ag6", T.ag[64:72, 1:2], 0.0), ("ag7", T.ag[96:104, 1:2], 0.0)):
+        vop(key, ["ag3"] if key == "ag4" else [], lambda: v.memset(view, val))
+    vop("tabn", ["tab"], lambda: v.tensor_scalar(T.tab[96:128, :], T.tab[96:128, :], 5, None, A.arith_shift_right))
+    vop("big", [], lambda: v.tensor_scalar(T.big[0:1, :], T.tab[0:1, 0:128], 0.0, BIG8 / 2048, A.mult, A.add))
+    vop("rhs", ["tabn"], lambda: v.tensor_scalar(T.rhs[:], T.tab[:], T.ag[:, 0:1], T.ag[:, 1:2], A.mult, A.add))
+    vop("qa", [LD], lambda: v.tensor_scalar(T.qi[64:80, 0:1], T.raw[64:80, 0:1], 6, None, A.arith_shift_right))
+    vop("qb", [], lambda: v.tensor_scalar(T.qi[96:104, 0:1], T.raw[96:104, 0:1], 63, None, A.bitwise_and))
+    vop("pd", [], lambda: v.tensor_scalar(T.par[0:64, :], T.raw[0:64, :], float(-CENTER), 1.0 / 2048, A.add, A.mult))
+    vop("pq", ["qb"], lambda: v.tensor_copy(T.par[64:128, 0:1], T.qi[64:128, 0:1]))
+
+    src_of = {0: T.par, 1: T.msg1, 2: T.msg2, 3: T.par}
+    col_of = {0: 0, 1: n - 1, 2: n - 2, 3: 1}
+    slot_of = {0: 0, 1: 1, 2: 2, 3: 0}
+
+    def lm(b):
+        c, s0, rows = col_of[b], 128 * slot_of[b], 64 if b == 3 else KROWS
+        return v.tensor_scalar(T.lm[0:rows, s0:s0 + 128], T.mask[0:rows, :], src_of[b][0:rows, c:c + 1], None, A.mult)
+
+    vop(("lm", 0), ["pq", "maskp"], lambda: lm(0))
+    vop("pa", [], lambda: v.tensor_scalar(T.par[96:104, 1:2], T.raw[96:104, 1:2], 1.0 / 4096, None, A.mult))
+    vop("pq2", [], lambda: v.tensor_scalar(T.par[64:128, 2:4], T.par[64:128, 2:4], T.par[64:128, 0:1], None, A.add))
+    vop("idh", ["idb"], lambda: v.tensor_copy(T.idh[:], T.cb[:, 0:128]))
+
+    def gather_deps(o):
+        b = o[1]
+        return [("conv", j) for j in job_of(b, o[2], o[3])] + [arr["xa"] if b == 3 else LDX]
+
+    def operand(o):
+        b = o[1]
+        win = T.xn if b == 3 else T.xw
+        return T["gb%d" % b][:, 16 * o[2]:16 * o[3]], win[:, 0:NS].indirect(T.off[:, 512 * b + o[2]:512 * b + o[3]])
+
+    def own_done(k):
+        return pairs(3, OWN[k][1], OWN[k][2]) + [("land", 1, k), ("land", 2, k)]
+
+    scalar_clipped = sum(2 * (OWN[o[1]][2] - OWN[o[1]][1]) for o in S_ORDER if o[0] == "clip")
+
+    for o in V_ORDER:
+        kind = o[0]
+        if kind == "pre2":
+            vop("nfold1", [], lambda: v.memset(T.nfold[:], -1.0))
+            vop("zb", [], lambda: v.memset(T.zb[:], 0.0))
+        elif kind == "pre3":
+            vop("t16b", ["t16"], lambda: v.tensor_scalar(T.t16b[:], T.t16[:], 15, None, A.bitwise_and))
+            vop("sel", ["t16b"], lambda: v.tensor_scalar(T.sel[:], T.t16b[:], 0.0, None, A.is_equal))
+        elif kind == "lm":
+            b = o[1]
+            vop(o, [("t", "0a"), ("t", "0b")] if b == 3 else [arr["m%d" % b]], lambda: lm(b))
+        elif kind == "sh":
+            b, lo, hi, bu, bt = JOBS[o[1]]
+            ac = 64 + slot_of[b]
+            vop(o, [("sq", o[1]), ("a", slot_of[b])], lambda: v.tensor_scalar(
+                T.shm[:, 512 * b + lo:512 * b + hi], T.sq[:, 512 * b + lo:512 * b + hi], T.py[:, ac:ac + 1],
+                LIFT - 4095.0 / 8192, A.mult, A.add))
+        elif kind == "conv":
+            b, lo, hi, bu, bt = JOBS[o[1]]
+            vop(o, [("add", o[1])], lambda: v.tensor_scalar(
+                T.off[:, 512 * b + lo:512 * b + hi], T[bt][:, lo:hi], BIG1 + CENTER - LIFT + 3.5, -BIG1, A.add, A.add))
+        elif kind == "g":
+            out, src = operand(o)
+            vop(o, gather_deps(o), lambda: v.tensor_copy(out, src))
+        elif kind == "clip":
+            bank, lo, hi = OWN[o[1]]
+            vop(o, own_done(o[1]), lambda: v.tensor_scalar(
+                T.clip[:, 128 * lo:128 * hi], T[bank][:, 0:128 * (hi - lo)], 255.0, None, A.min))
+        elif kind == "end":
+            vop(o, [("sum", 0), ("sum", 1), ("sum", 2)], lambda: v.tensor_scalar(
+                T.ysb[:], T.py[:, 0:64], 255.0 * scalar_clipped, None, A.add))
+
+    s = g.scalar
+    for o in S_ORDER:
+        kind = o[0]
+        if kind == "sq":
+            b, lo, hi, bu, bt = JOBS[o[1]]
+            wait("s", [("u", o[1])])
+            mark("s", s.activation(T.sq[:, 512 * b + lo:512 * b + hi], T[bu][:, lo:hi], F.Square,
+                                   bias=CENTER / 8 - BIG8 / 8, scale=0.125), o)
+        elif kind == "g":
+            out, src = operand(o)
+            wait("s", gather_deps(o))
+            mark("s", s.activation(out, src, F.Copy), o)
+        elif kind == "ev":
+            b, k = o[1], o[2]
+            wait("s", pairs(b, 4 * k, 4 * k + 4))
+            mark("s", s.activation(T["out%d" % b][:, 512 * k:512 * k + 512], T["pr%d" % k][:], F.Copy), o)
+        elif kind == "clip":
+            bank, lo, hi = OWN[o[1]]
+            wait("s", own_done(o[1]))
+            mark("s", s.activation(T.clip[:, 128 * lo:128 * hi], T[bank][:, 0:128 * (hi - lo)], F.Relu,
+                                   bias=255.0, scale=-1.0), o)
+
+    p = g.tensor
+    bank_free = {"0a": [], "0b": [], "3": [("sq", "0a"), ("conv", "0a")], "1a": [("sq", "0b"), ("conv", "0b")],
+                 "1b": [("sq", "3"), ("conv", "3")], "2": [("sq", "1b"), ("conv", "1b")]}
+
+    def own_bank(m):
+        return [k for k, w in enumerate(OWN) if w[1] <= m < w[2]][0]
+
+    last_own = {}
+    for o in P_ORDER:
+        if o[0] == "r" and o[1] == 3:
+            last_own[own_bank(o[2])] = o
+        elif o[0] == "land":
+            last_own[o[2]] = o
+    sums = [o for o in P_ORDER if o[0] == "sum"]
+    for o in P_ORDER:
+        kind = o[0]
+        if kind == "a":
+            b = o[1]
+            wait("p", {0: ["pa"], 1: [arr["m1"], ("sh", "0b"), ("sh", "3")],
+                       2: [arr["m2"], ("sh", "1a"), ("sh", "1b")]}[b])
+            ins = p.matmul(T.py[:, 64 + b:65 + b], T.mask[64:104, :], src_of[b][64:104, 1:2], True, True)
+        elif kind in ("u", "t"):
+            b, lo, hi, bu, bt = JOBS[o[1]]
+            s0 = 128 * slot_of[b]
+            wait("p", [("lm", b)] + bank_free[o[1]])
+            bank = T[bu if kind == "u" else bt]
+            ins = p.matmul(bank[:, lo:hi], T.lm[0:KROWS, s0:s0 + 128], T.rhs[0:KROWS, lo:hi], True, False)
+            if kind == "u":
+                ins = p.matmul(bank[:, lo:hi], T.big[0:1, :], T.rhs[0:1, lo:hi], False, True)
+        elif kind == "add":
+            b, lo, hi, bu, bt = JOBS[o[1]]
+            wait("p", [("sh", o[1]), "idh"])
+            ins = p.matmul(T[bt][:, lo:hi], T.idh[:], T.shm[:, 512 * b + lo:512 * b + hi], False, True)
+        elif kind == "open":
+            wait("p", gathers(0, 0, 32) + ["zb"])
+            for bank, lo, hi in OWN:
+                ins = p.matmul(T[bank][:, 0:128 * (hi - lo)], T.zb[:], T.gb0[:, 0:128 * (hi - lo)], True, False)
+        elif kind == "r":
+            b, m = o[1], o[2]
+            deps = gathers(b, 64 * m, 64 * m + 64) + ["sel"]
+            alone = b in (1, 2)
+            if alone:
+                bank, c0, final = "pr%d" % (m // 4), 128 * (m % 4), False
+                deps += [("sq", "1a"), ("conv", "1a")] + ([("ev", 1, m // 4)] if b == 2 else [])
+            else:
+                k = own_bank(m)
+                bank, c0, final = OWN[k][0], 128 * (m - OWN[k][1]), last_own[k] == o
+            wait("p", deps)
+            for t in range(8):
+                ins = p.matmul(T[bank][:, c0 + 16 * t:c0 + 16 * t + 16],
+                               T["gb%d" % b][:, 1024 * m + t:1024 * m + 1024:8], T.sel[:],
+                               alone, alone or (final and t == 7))
+        elif kind == "land":
+            b, k = o[1], o[2]
+            bank, lo, hi = OWN[k]
+            wait("p", [arr["l%d%s" % (b, "a" if k == 0 else "b")], "idb"])
+            ins = p.matmul(T[bank][:, 0:128 * (hi - lo)], T.cb[:, 0:128], T["land%d" % b][:, 128 * lo:128 * hi],
+                           False, last_own[k] == o)
+        elif kind == "sum":
+            k = o[1]
+            bank, lo, hi = OWN[k]
+            wait("p", [("clip", k), ("sh", "2"), "nf1"])
+            fold = T.nfold[:] if ("clip", k) in S_ORDER else T.cb[:, 128:192]
+            for m in range(lo, hi):
+                ins = p.matmul(T.py[:, 0:64], T.clip[:, 128 * m:128 * m + 128], fold,
+                               o == sums[0] and m == lo, o == sums[-1] and m == hi - 1)
+        mark("p", ins, o)
+
+    wait("y", [("end",)])
+    g.sync.dma_start(T.y[:, :], T.ysb[:]).then_inc(sem.st, 16)
+    g.sync.wait_ge(sem.st, 16)
+    wait("g", [("sent", sent[0]), ("sg", counts["sg"]), ("ss", counts["ss"]), ("sp", counts["sp"])])

@@ -1,49 +1,42 @@
-from concourse.bass import DstId, RemoteDMATransfer
 from concourse.mybir import AluOpType, ActivationFunctionType
 
+SIM_CORES = 64
 NS = 2560
-HALF = NS // 2
+C1, CA, E0, EM, E1 = 1664, 2112, 896, 1216, 1536
 CENTER = 1280
 BIG8 = 1.5 * 2.0 ** 26
-BIG1 = 2.0 ** 23
-LIFT = 1536
-KROWS = 105
+BIG1 = 1.5 * 2.0 ** 23
+KROWS = 106
 
 SCRATCH = {}
 for _dt, _bufs in (
         ("int32", dict(raw=4, qi=4, tab=512, t16=16, t16b=16)),
-        ("float32", dict(par=4, msg1=4, msg2=4, ag=4, mask=128, sq=2048, ysb=64)),
-        ("float16", dict(rhs=512, lm=384, big=128, idh=128, shm=2048)),
+        ("float32", dict(par=4, msg1=4, ag=4, mask=128, dg=256, sq=2048, ysb=64)),
+        ("float16", dict(rhs=512, lm=256, big=384)),
         ("uint16", dict(off=2048)),
-        ("bfloat16", dict(sel=16, cb=192, nfold=64, zb=128, xw=NS, xn=NS, xh=HALF, gb0=8192, gb1=8192, gb2=8192,
-                          gb3=8192, out1=1024, out2=1024, land1=1024, land2=1024, clip=1024))):
+        ("bfloat16", dict(sel=16, cb=192, nfold=64, zb=128, xw=NS, xn=NS, xm=NS, xh=NS, gb0=8192, gb1=8192, gb2=8192,
+                          gb3=8192, out1=1024, land1=1024, clip=1024))):
     for _k, _w in _bufs.items():
         SCRATCH[_k] = ("sbuf", [128, _w], _dt)
 for _k in ("pu", "pt", "pr0", "pr1", "po0", "po1", "po2", "py"):
     SCRATCH[_k] = ("psum", [128, 512], "float32")
-SEMAPHORES = ["sv", "ss", "sp", "sg", "ld", "ldx", "st", "sent", "m1", "m2", "xa", "hx",
-              "l1a", "l1b", "l2a", "l2b"]
+SEMAPHORES = ["sv", "ss", "sp", "sg", "ld", "ldx", "st", "sent", "m1", "xa", "xb", "hx", "hy", "l1a", "l1b"]
 
-JOBS = {"0a": (0, 0, 128, "pu", "pt"), "0b": (0, 128, 512, "pr0", "pr1"), "3": (3, 0, 512, "pu", "pt"),
-        "1a": (1, 0, 128, "pr0", "pr1"), "1b": (1, 128, 512, "pu", "pt"), "2": (2, 0, 512, "pu", "pt")}
+JOBS = {"0a": (0, 0, 192, "pu", "pt"), "0b": (0, 192, 512, "pr0", "pr1"), "2": (2, 0, 512, "pu", "pt"),
+        "1a": (1, 0, 128, "pr0", "pr1"), "1b": (1, 128, 512, "po0", "po1"), "3": (3, 0, 512, "pu", "pt")}
 
 V_ORDER = [
-    ("sh", "0a"), ("pre2",), ("conv", "0a"), ("sh", "0b"), ("pre3",), ("conv", "0b"),
-    ("g", 0, 120, 176), ("lm", 3), ("g", 0, 224, 320), ("sh", "3"), ("g", 0, 376, 400), ("conv", "3"),
-    ("lm", 1), ("g", 0, 456, 488), ("sh", "1a"), ("conv", "1a"), ("sh", "1b"), ("g", 1, 96, 112), ("conv", "1b"),
-    ("g", 1, 112, 160), ("lm", 2), ("g", 1, 224, 320), ("sh", "2"), ("g", 1, 376, 416), ("conv", "2"),
-    ("g", 1, 456, 512),
-    ("g", 2, 80, 144), ("g", 2, 208, 280), ("g", 2, 336, 400), ("g", 2, 456, 512),
-    ("g", 3, 48, 128), ("g", 3, 200, 280), ("g", 3, 352, 448), ("g", 3, 448, 480),
-    ("clip", 2), ("end",),
+    ("dg", 0), ("pre2",), ("conv", "0a"), ("pre3",), ("g", 0, 80, 144), ("conv", "0b"), ("lm", 2),
+    ("g", 0, 192, 280), ("g", 0, 344, 384), ("lm", 1), ("dg", 1), ("g", 0, 416, 464),
+    ("conv", "1a"), ("g", 1, 80, 120), ("conv", "1b"), ("lm", 3), ("g", 1, 200, 296), ("conv", "2"),
+    ("g", 1, 400, 512), ("g", 2, 104, 256), ("conv", "3"), ("g", 2, 392, 512),
+    ("g", 3, 136, 256), ("g", 3, 336, 456), ("g", 3, 456, 488), ("clip", 2), ("end",),
 ]
 S_ORDER = [
-    ("sq", "0a"), ("sq", "0b"), ("g", 0, 0, 120), ("g", 0, 176, 224), ("sq", "3"), ("g", 0, 320, 376),
-    ("g", 0, 400, 456), ("sq", "1a"), ("sq", "1b"), ("g", 0, 488, 512),
-    ("g", 1, 0, 96), ("g", 1, 160, 224), ("sq", "2"), ("g", 1, 320, 376), ("ev", 1, 0), ("g", 1, 416, 456),
-    ("g", 2, 0, 80), ("ev", 1, 1), ("g", 2, 144, 208), ("g", 2, 280, 336), ("ev", 2, 0), ("g", 2, 400, 456),
-    ("g", 3, 0, 48), ("ev", 2, 1), ("g", 3, 128, 200), ("g", 3, 280, 352), ("clip", 0), ("g", 3, 480, 512),
-    ("clip", 1),
+    ("sq", "0a"), ("sq", "0b"), ("g", 0, 0, 80), ("g", 0, 144, 192), ("sq", "2"), ("g", 0, 280, 344),
+    ("g", 0, 384, 416), ("sq", "1a"), ("sq", "1b"), ("g", 0, 464, 512), ("g", 1, 0, 80), ("g", 1, 120, 200),
+    ("g", 1, 296, 400), ("sq", "3"), ("ev", 1, 0), ("g", 2, 0, 104), ("ev", 1, 1), ("g", 2, 256, 392),
+    ("g", 3, 0, 136), ("g", 3, 256, 336), ("clip", 0), ("g", 3, 488, 512), ("clip", 1),
 ]
 
 
@@ -52,13 +45,13 @@ def pairs(b, lo, hi):
 
 
 P_ORDER = (
-    [("u", "0a"), ("a", 0), ("u", "0b"), ("t", "0a"), ("add", "0a"), ("t", "0b"), ("add", "0b"),
-     ("u", "3"), ("t", "3"), ("open",)] + pairs(0, 0, 3) + [("add", "3")] + pairs(0, 3, 5)
-    + [("u", "1a"), ("a", 1), ("u", "1b"), ("t", "1a"), ("add", "1a"), ("t", "1b"), ("add", "1b")]
-    + pairs(0, 5, 8) + pairs(1, 0, 2) + [("u", "2"), ("a", 2), ("t", "2")] + pairs(1, 2, 4) + [("add", "2")]
-    + pairs(1, 4, 8) + pairs(2, 0, 8)
-    + [("land", 1, 0), ("land", 1, 1), ("land", 1, 2)] + pairs(3, 0, 4) + [("land", 2, 0)] + pairs(3, 4, 7)
-    + [("land", 2, 1), ("land", 2, 2), ("sum", 0), ("r", 3, 7), ("sum", 2), ("sum", 1)]
+    [("u", "0a"), ("a", 0), ("t", "0a"), ("add", "0a"), ("u", "0b"), ("t", "0b"), ("add", "0b"),
+     ("u", "2"), ("t", "2"),
+     ("a", 1), ("u", "1a"), ("t", "1a"), ("u", "1b"), ("add", "1a"), ("t", "1b"), ("add", "1b"), ("add", "2"),
+     ("u", "3")] + pairs(1, 0, 4) + [("t", "3")] + pairs(1, 4, 8) + [("add", "3"), ("open",)]
+    + pairs(0, 0, 8) + pairs(2, 0, 8) + pairs(3, 0, 4)
+    + [("land", 1, 0), ("land", 1, 1), ("land", 1, 2)] + pairs(3, 4, 7)
+    + [("sum", 0), ("r", 3, 7), ("sum", 2), ("sum", 1)]
 )
 OWN = [("po0", 0, 4), ("po1", 4, 7), ("po2", 7, 8)]
 
@@ -67,11 +60,50 @@ def bits(engines):
     return sum(1 << e for e in engines)
 
 
-def helper_of(core, T, topo, dst):
-    for c in topo.cores_of(core):
-        if topo.die(c) != topo.die(core) and T.rank_of(c) is None and topo.may_write(c, dst):
-            return c
-    return None
+def helpers_of(r, T, topo):
+    cores = list(T.cores)
+    core, one, two = cores[r % len(cores)], cores[(r - 1) % len(cores)], cores[(r - 2) % len(cores)]
+    free = [c for c in topo.cores_of(core) if T.rank_of(c) is None]
+    other = [c for c in free if topo.die(c) != topo.die(core) and topo.may_write(c, one) and topo.may_write(c, two)][0]
+    last = [c for c in range(SIM_CORES) if topo.mates(topo.chip(c), topo.chip(two)) and T.rank_of(c) is None
+            and topo.die(c) == topo.die(core) and topo.may_write(c, two)][0]
+    port = [c for c in free if topo.die(c) == topo.die(core) and topo.may_write(c, last)][0]
+    return other, port, last
+
+
+def near_engines(r, helper, T, topo):
+    cores = list(T.cores)
+    core = cores[r % len(cores)]
+    return [e for e in topo.engines(core, helper) if e not in topo.engines(core, cores[(r - 1) % len(cores)])]
+
+
+def hand_on(g, core, T, topo):
+    cores = list(T.cores)
+    n = len(cores)
+    for r in range(n):
+        other, port, last = helpers_of(r, T, topo)
+        one, two = cores[(r - 1) % n], cores[(r - 2) % n]
+        if core == other:
+            k = len(near_engines(r, core, T, topo))
+            steps = [(("hx", k), T.xn, "xa", CA, NS, one), (("hy", k), T.xn, "xa", C1, CA, one),
+                     (None, T.xm, "xb", E1, NS, two)]
+        elif core == port:
+            steps = [(("hx", len(near_engines(r, core, T, topo))), T.xh, "hx", E0, EM, last),
+                     (None, T.xh, "hy", EM, E1, last)]
+        elif core == last:
+            k = len(topo.engines(port, core))
+            steps = [(("hx", k), T.xm, "xb", E0, EM, two), (("hy", k), T.xm, "xb", EM, E1, two)]
+        else:
+            continue
+        total = 0
+        for need, win, arrive, lo, hi, to in steps:
+            mine = topo.engines(core, to)
+            rid, pid, _ = topo.addr(to)
+            if need:
+                g.wait_ge(T.sem[need[0]], need[1])
+            g.remote_dma(win[:, lo:hi], T.xh[:, lo:hi], T.sem[arrive], T.sem.sent, pid, rid, bits(mine))
+            total += len(mine)
+        g.wait_ge(T.sem.sent, total)
 
 
 def rank_program(g, core, T, topo):
@@ -80,16 +112,7 @@ def rank_program(g, core, T, topo):
     rank = T.rank_of(core)
     sem = T.sem
     if rank is None:
-        for r in range(n):
-            dst = cores[(r - 1) % n]
-            if helper_of(cores[r], T, topo, dst) == core:
-                far = topo.engines(cores[r], dst)
-                near = [e for e in topo.engines(cores[r], core) if e not in far]
-                mine = topo.engines(core, dst)
-                rid, pid, _ = topo.addr(dst)
-                g.wait_ge(sem.hx, len(near))
-                g.remote_dma(T.xn[:, HALF:NS], T.xh[:], sem.xa, sem.sent, pid, rid, bits(mine))
-                g.wait_ge(sem.sent, len(mine))
+        hand_on(g, core, T, topo)
         return
 
     A = AluOpType
@@ -120,14 +143,14 @@ def rank_program(g, core, T, topo):
     def far_engines(src, dst):
         return topo.engines(cores[src % n], cores[dst % n])
 
-    h_in = helper_of(cores[(q + 1) % n], T, topo, core)
-    arr = {"m1": q + 1, "m2": q + 2, "l1a": q - 1, "l1b": q - 1, "l2a": q - 2, "l2b": q - 2}
-    arr = {k: (k, len(far_engines(r, q))) for k, r in arr.items()}
-    arr["xa"] = ("xa", len(far_engines(q + 1, q)) + len(topo.engines(h_in, core)))
+    arr = {k: (k, len(far_engines(r, q))) for k, r in (("m1", q + 1), ("l1a", q - 1), ("l1b", q - 1))}
+    arr["xa"] = ("xa", len(far_engines(q + 1, q)) + 2 * len(topo.engines(helpers_of(q + 1, T, topo)[0], core)))
+    other2, _, last2 = helpers_of(q + 2, T, topo)
+    arr["xb"] = ("xb", len(far_engines(q + 2, q)) + len(topo.engines(other2, core)) + 2 * len(topo.engines(last2, core)))
     LD, LDX = ("ld", 7 * 16), ("ldx", 8 * 16)
 
-    v_keys = ["mask1", "cb1", "qi1", "ag0", "ag1", "ag2", "ag3", "par0", "ag4", "ag5", "ag6", "ag7",
-              "tabn", "big", "rhs", "qa", "qb", "pd", "pq", ("lm", 0), "pa", "pq2", "idh"]
+    v_keys = ["mask1", "cb1", "qi1", "ag0", "ag1", "ag2", "ag3", "ag8", "par0", "ag4", "ag5", "ag6", "ag9", "ag10",
+              "ag7", "tabn", "big", "up", "rhs", "qa", "qb", "pd", "pq", ("lm", 0), "pa", "pq2", "down", "half"]
     for o in V_ORDER:
         v_keys += {"pre2": ["nfold1", "zb"], "pre3": ["t16b", "sel"]}.get(o[0], [o])
     g_keys = ["tab", "maskd", "maskq", "maskp", "idb", "t16", "f0", "f1", "nf0", "nf1"]
@@ -159,6 +182,12 @@ def rank_program(g, core, T, topo):
         g.remote_dma(out_ap, in_ap, sem[name], sem.sent, pid, rid, bits(eng))
         sent[0] += len(eng)
 
+    def copy_to(helper, name, lo, hi):
+        eng = near_engines(q, helper, T, topo)
+        rid, pid, _ = topo.addr(helper)
+        g.remote_dma(T.xh[:, lo:hi], T.xw[:, lo:hi], sem[name], sem.sent, pid, rid, bits(eng))
+        sent[0] += len(eng)
+
     def gop(key, deps, make):
         wait("g", deps + [("sg", counts["sg"])])
         mark("g", make(), key)
@@ -171,33 +200,22 @@ def rank_program(g, core, T, topo):
     pick("maskq", [], T.mask[64:96, :], [[0, 8], [-8, 2], [-1, 8]])
     pick("maskp", [], T.mask[96:104, :], [[0, 16], [-1, 8]])
     pick("idb", ["cb1"], T.cb[:, 0:128], [[-1, 128]])
-    gop("t16", [], lambda: g.iota(T.t16[:], [[-1, 16]], 16, 1))
     wait("g", ["pq2"])
     send(T.msg1[:], T.par[:], "m1", q - 1)
-    send(T.msg2[:], T.par[:], "m2", q + 2)
-    to = cores[(q - 1) % n]
-    h_out = helper_of(core, T, topo, to)
-    far = topo.engines(core, to)
-    near = [e for e in topo.engines(core, h_out) if e not in far]
-    rid, pid, _ = topo.addr(to)
-    hrid, hpid, _ = topo.addr(h_out)
+    gop("t16", [], lambda: g.iota(T.t16[:], [[-1, 16]], 16, 1))
+    other, port, _ = helpers_of(q, T, topo)
     wait("g", [LDX])
-    g.remote_dma_fused([
-        RemoteDMATransfer(dst_ids=[DstId(rid=rid, pnc=pid)], dma_engine_mask=bits(far), remote_sem=sem.xa,
-                          src=T.xw[:, 0:HALF], dst=T.xn[:, 0:HALF]),
-        RemoteDMATransfer(dst_ids=[DstId(rid=hrid, pnc=hpid)], dma_engine_mask=bits(near), remote_sem=sem.hx,
-                          src=T.xw[:, HALF:NS], dst=T.xh[:]),
-    ], local_sem=sem.sent)
-    sent[0] += len(far) + len(near)
+    copy_to(other, "hx", CA, NS)
+    send(T.xn[:, 0:C1], T.xw[:, 0:C1], "xa", q - 1)
+    copy_to(other, "hy", E1, CA)
+    copy_to(port, "hx", E0, E1)
+    send(T.xm[:, 0:E0], T.xw[:, 0:E0], "xb", q - 2)
     for key, view in (("f0", T.cb[0:64, 128:192]), ("f1", T.cb[64:128, 128:192]),
                       ("nf0", T.nfold[0:64, :]), ("nf1", T.nfold[64:128, :])):
         pick(key, ["nfold1"], view, [[-1, 64]])
-    for o in S_ORDER:
-        if o[0] == "ev":
-            b, k = o[1], o[2]
-            wait("g", [o])
-            send(T["land%d" % b][:, 512 * k:512 * k + 512], T["out%d" % b][:, 512 * k:512 * k + 512],
-                 "l%d%s" % (b, "ab"[k]), q + b)
+    for k in range(2):
+        wait("g", [("ev", 1, k)])
+        send(T.land1[:, 512 * k:512 * k + 512], T.out1[:, 512 * k:512 * k + 512], "l1" + "ab"[k], q + 1)
 
     v = g.vector
 
@@ -208,42 +226,52 @@ def rank_program(g, core, T, topo):
     for key, view, val in (
             ("mask1", T.mask[:], 1.0), ("cb1", T.cb[:], 1.0), ("qi1", T.qi[64:128, :], 1),
             ("ag0", T.ag[:, 0:1], 0.0), ("ag1", T.ag[0:64, 1:2], 2048.0), ("ag2", T.ag[64:96, 1:2], 1.0 / 256),
-            ("ag3", T.ag[96:128, 1:2], -2047.0 / 512), ("par0", T.par[64:128, :], 0.0),
+            ("ag3", T.ag[96:128, 1:2], 3.5), ("ag8", T.ag[64:KROWS, 2:3], -585.0 / 4096),
+            ("par0", T.par[64:128, :], 0.0),
             ("ag4", T.ag[64:80, 0:1], 2.0 / 256), ("ag5", T.ag[96:104, 0:1], 1.0 / 256),
-            ("ag6", T.ag[64:72, 1:2], 0.0), ("ag7", T.ag[96:104, 1:2], 0.0)):
-        vop(key, ["ag3"] if key == "ag4" else [], lambda: v.memset(view, val))
+            ("ag6", T.ag[64:72, 1:2], 0.0), ("ag9", T.ag[96:105, 1:2], -2047.0 / 512),
+            ("ag10", T.ag[64:105, 2:3], 0.0), ("ag7", T.ag[96:104, 1:2], 0.0)):
+        vop(key, {"ag4": ["ag8"], "ag7": ["ag9"]}.get(key, []), lambda: v.memset(view, val))
+
+    def row(key, i, val):
+        vop(key, [], lambda: v.tensor_scalar(T.big[0:1, 128 * i:128 * i + 128], T.tab[0:1, 0:128], 0.0, val / 2048,
+                                             A.mult, A.add))
+
     vop("tabn", ["tab"], lambda: v.tensor_scalar(T.tab[96:128, :], T.tab[96:128, :], 5, None, A.arith_shift_right))
-    vop("big", [], lambda: v.tensor_scalar(T.big[0:1, :], T.tab[0:1, 0:128], 0.0, BIG8 / 2048, A.mult, A.add))
+    row("big", 0, BIG8)
+    row("up", 1, BIG1)
     vop("rhs", ["tabn"], lambda: v.tensor_scalar(T.rhs[:], T.tab[:], T.ag[:, 0:1], T.ag[:, 1:2], A.mult, A.add))
     vop("qa", [LD], lambda: v.tensor_scalar(T.qi[64:80, 0:1], T.raw[64:80, 0:1], 6, None, A.arith_shift_right))
     vop("qb", [], lambda: v.tensor_scalar(T.qi[96:104, 0:1], T.raw[96:104, 0:1], 63, None, A.bitwise_and))
     vop("pd", [], lambda: v.tensor_scalar(T.par[0:64, :], T.raw[0:64, :], float(-CENTER), 1.0 / 2048, A.add, A.mult))
     vop("pq", ["qb"], lambda: v.tensor_copy(T.par[64:128, 0:1], T.qi[64:128, 0:1]))
 
-    src_of = {0: T.par, 1: T.msg1, 2: T.msg2, 3: T.par}
-    col_of = {0: 0, 1: n - 1, 2: n - 2, 3: 1}
-    slot_of = {0: 0, 1: 1, 2: 2, 3: 0}
+    src_of = {0: T.par, 1: T.msg1, 2: T.par, 3: T.par}
+    col_of = {0: 0, 1: n - 1, 2: 1, 3: 2}
+    slot_of = {0: 0, 1: 1, 2: 0, 3: 0}
 
     def lm(b):
-        c, s0, rows = col_of[b], 128 * slot_of[b], 64 if b == 3 else KROWS
+        c, s0, rows = col_of[b], 128 * slot_of[b], 64 if b >= 2 else KROWS
         return v.tensor_scalar(T.lm[0:rows, s0:s0 + 128], T.mask[0:rows, :], src_of[b][0:rows, c:c + 1], None, A.mult)
 
     vop(("lm", 0), ["pq", "maskp"], lambda: lm(0))
     vop("pa", [], lambda: v.tensor_scalar(T.par[96:104, 1:2], T.raw[96:104, 1:2], 1.0 / 4096, None, A.mult))
-    vop("pq2", [], lambda: v.tensor_scalar(T.par[64:128, 2:4], T.par[64:128, 2:4], T.par[64:128, 0:1], None, A.add))
-    vop("idh", ["idb"], lambda: v.tensor_copy(T.idh[:], T.cb[:, 0:128]))
+    vop("pq2", [], lambda: v.tensor_copy(T.par[64:128, 3:4], T.qi[64:128, 0:1]))
+    row("down", 2, -BIG1)
+    vop("half", [], lambda: v.tensor_scalar(T.big[64:KROWS, 0:128], T.tab[64:KROWS, 0:128], 0.0, T.ag[64:KROWS, 2:3],
+                                            A.mult, A.add))
 
     def gather_deps(o):
         b = o[1]
-        return [("conv", j) for j in job_of(b, o[2], o[3])] + [arr["xa"] if b == 3 else LDX]
+        return [("conv", j) for j in job_of(b, o[2], o[3])] + [{2: arr["xa"], 3: arr["xb"]}.get(b, LDX)]
 
     def operand(o):
         b = o[1]
-        win = T.xn if b == 3 else T.xw
+        win = {2: T.xn, 3: T.xm}.get(b, T.xw)
         return T["gb%d" % b][:, 16 * o[2]:16 * o[3]], win[:, 0:NS].indirect(T.off[:, 512 * b + o[2]:512 * b + o[3]])
 
     def own_done(k):
-        return pairs(3, OWN[k][1], OWN[k][2]) + [("land", 1, k), ("land", 2, k)]
+        return pairs(3, OWN[k][1], OWN[k][2]) + [("land", 1, k)]
 
     scalar_clipped = sum(2 * (OWN[o[1]][2] - OWN[o[1]][1]) for o in S_ORDER if o[0] == "clip")
 
@@ -257,17 +285,15 @@ def rank_program(g, core, T, topo):
             vop("sel", ["t16b"], lambda: v.tensor_scalar(T.sel[:], T.t16b[:], 0.0, None, A.is_equal))
         elif kind == "lm":
             b = o[1]
-            vop(o, [("t", "0a"), ("t", "0b")] if b == 3 else [arr["m%d" % b]], lambda: lm(b))
-        elif kind == "sh":
-            b, lo, hi, bu, bt = JOBS[o[1]]
-            ac = 64 + slot_of[b]
-            vop(o, [("sq", o[1]), ("a", slot_of[b])], lambda: v.tensor_scalar(
-                T.shm[:, 512 * b + lo:512 * b + hi], T.sq[:, 512 * b + lo:512 * b + hi], T.py[:, ac:ac + 1],
-                LIFT - 4095.0 / 8192, A.mult, A.add))
+            vop(o, {1: [arr["m1"]], 2: [("t", "0a"), ("t", "0b")], 3: [("t", "2")]}[b], lambda: lm(b))
+        elif kind == "dg":
+            b = o[1]
+            vop(o, [("a", b), "idb"], lambda: v.tensor_scalar(
+                T.dg[:, 128 * b:128 * b + 128], T.cb[:, 0:128], T.py[:, 64 + b:65 + b], None, A.mult))
         elif kind == "conv":
             b, lo, hi, bu, bt = JOBS[o[1]]
             vop(o, [("add", o[1])], lambda: v.tensor_scalar(
-                T.off[:, 512 * b + lo:512 * b + hi], T[bt][:, lo:hi], BIG1 + CENTER - LIFT + 3.5, -BIG1, A.add, A.add))
+                T.off[:, 512 * b + lo:512 * b + hi], T[bt][:, lo:hi], BIG1, CENTER - BIG1, A.add, A.add))
         elif kind == "g":
             out, src = operand(o)
             vop(o, gather_deps(o), lambda: v.tensor_copy(out, src))
@@ -292,9 +318,9 @@ def rank_program(g, core, T, topo):
             wait("s", gather_deps(o))
             mark("s", s.activation(out, src, F.Copy), o)
         elif kind == "ev":
-            b, k = o[1], o[2]
-            wait("s", pairs(b, 4 * k, 4 * k + 4))
-            mark("s", s.activation(T["out%d" % b][:, 512 * k:512 * k + 512], T["pr%d" % k][:], F.Copy), o)
+            k = o[2]
+            wait("s", pairs(1, 4 * k, 4 * k + 4))
+            mark("s", s.activation(T.out1[:, 512 * k:512 * k + 512], T["pr%d" % k][:], F.Copy), o)
         elif kind == "clip":
             bank, lo, hi = OWN[o[1]]
             wait("s", own_done(o[1]))
@@ -302,8 +328,8 @@ def rank_program(g, core, T, topo):
                                    bias=255.0, scale=-1.0), o)
 
     p = g.tensor
-    bank_free = {"0a": [], "0b": [], "3": [("sq", "0a"), ("conv", "0a")], "1a": [("sq", "0b"), ("conv", "0b")],
-                 "1b": [("sq", "3"), ("conv", "3")], "2": [("sq", "1b"), ("conv", "1b")]}
+    bank_free = {"0a": [], "0b": [], "2": [("sq", "0a"), ("conv", "0a")], "1a": [("sq", "0b"), ("conv", "0b")],
+                 "1b": [], "3": [("sq", "2"), ("conv", "2")]}
 
     def own_bank(m):
         return [k for k, w in enumerate(OWN) if w[1] <= m < w[2]][0]
@@ -319,32 +345,38 @@ def rank_program(g, core, T, topo):
         kind = o[0]
         if kind == "a":
             b = o[1]
-            wait("p", {0: ["pa"], 1: [arr["m1"], ("sh", "0b"), ("sh", "3")],
-                       2: [arr["m2"], ("sh", "1a"), ("sh", "1b")]}[b])
+            wait("p", {0: ["pa"], 1: [arr["m1"], ("dg", 0)]}[b])
             ins = p.matmul(T.py[:, 64 + b:65 + b], T.mask[64:104, :], src_of[b][64:104, 1:2], True, True)
-        elif kind in ("u", "t"):
+        elif kind == "u":
             b, lo, hi, bu, bt = JOBS[o[1]]
             s0 = 128 * slot_of[b]
             wait("p", [("lm", b)] + bank_free[o[1]])
-            bank = T[bu if kind == "u" else bt]
-            ins = p.matmul(bank[:, lo:hi], T.lm[0:KROWS, s0:s0 + 128], T.rhs[0:KROWS, lo:hi], True, False)
-            if kind == "u":
-                ins = p.matmul(bank[:, lo:hi], T.big[0:1, :], T.rhs[0:1, lo:hi], False, True)
+            p.matmul(T[bu][:, lo:hi], T.lm[0:KROWS - 1, s0:s0 + 128], T.rhs[0:KROWS - 1, lo:hi], True, False)
+            ins = p.matmul(T[bu][:, lo:hi], T.big[0:1, 0:128], T.rhs[0:1, lo:hi], False, True)
+        elif kind == "t":
+            b, lo, hi, bu, bt = JOBS[o[1]]
+            s0 = 128 * slot_of[b]
+            wait("p", [("lm", b), "half"] + bank_free[o[1]])
+            p.matmul(T[bt][:, lo:hi], T.lm[0:KROWS, s0:s0 + 128], T.rhs[0:KROWS, lo:hi], True, False)
+            p.matmul(T[bt][:, lo:hi], T.big[0:1, 128:256], T.rhs[0:1, lo:hi], False, False)
+            p.matmul(T[bt][:, lo:hi], T.big[0:1, 256:384], T.rhs[0:1, lo:hi], False, False)
+            ins = p.matmul(T[bt][:, lo:hi], T.big[64:KROWS, 0:128], T.rhs[64:KROWS, lo:hi], False, False)
         elif kind == "add":
             b, lo, hi, bu, bt = JOBS[o[1]]
-            wait("p", [("sh", o[1]), "idh"])
-            ins = p.matmul(T[bt][:, lo:hi], T.idh[:], T.shm[:, 512 * b + lo:512 * b + hi], False, True)
+            s0 = 128 * slot_of[b]
+            wait("p", [("sq", o[1]), ("dg", slot_of[b])])
+            ins = p.matmul(T[bt][:, lo:hi], T.dg[:, s0:s0 + 128], T.sq[:, 512 * b + lo:512 * b + hi], False, True)
         elif kind == "open":
-            wait("p", gathers(0, 0, 32) + ["zb"])
+            wait("p", gathers(0, 0, 32) + ["zb", ("sq", "1b"), ("conv", "1b")])
             for bank, lo, hi in OWN:
                 ins = p.matmul(T[bank][:, 0:128 * (hi - lo)], T.zb[:], T.gb0[:, 0:128 * (hi - lo)], True, False)
         elif kind == "r":
             b, m = o[1], o[2]
             deps = gathers(b, 64 * m, 64 * m + 64) + ["sel"]
-            alone = b in (1, 2)
+            alone = b == 1
             if alone:
                 bank, c0, final = "pr%d" % (m // 4), 128 * (m % 4), False
-                deps += [("sq", "1a"), ("conv", "1a")] + ([("ev", 1, m // 4)] if b == 2 else [])
+                deps += [("sq", "1a"), ("conv", "1a")]
             else:
                 k = own_bank(m)
                 bank, c0, final = OWN[k][0], 128 * (m - OWN[k][1]), last_own[k] == o
@@ -354,15 +386,15 @@ def rank_program(g, core, T, topo):
                                T["gb%d" % b][:, 1024 * m + t:1024 * m + 1024:8], T.sel[:],
                                alone, alone or (final and t == 7))
         elif kind == "land":
-            b, k = o[1], o[2]
+            k = o[2]
             bank, lo, hi = OWN[k]
-            wait("p", [arr["l%d%s" % (b, "a" if k == 0 else "b")], "idb"])
-            ins = p.matmul(T[bank][:, 0:128 * (hi - lo)], T.cb[:, 0:128], T["land%d" % b][:, 128 * lo:128 * hi],
+            wait("p", [arr["l1a" if k == 0 else "l1b"], "idb"])
+            ins = p.matmul(T[bank][:, 0:128 * (hi - lo)], T.cb[:, 0:128], T.land1[:, 128 * lo:128 * hi],
                            False, last_own[k] == o)
         elif kind == "sum":
             k = o[1]
             bank, lo, hi = OWN[k]
-            wait("p", [("clip", k), ("sh", "2"), "nf1"])
+            wait("p", [("clip", k), ("dg", 1), "nf1"])
             fold = T.nfold[:] if ("clip", k) in S_ORDER else T.cb[:, 128:192]
             for m in range(lo, hi):
                 ins = p.matmul(T.py[:, 0:64], T.clip[:, 128 * m:128 * m + 128], fold,

@@ -10,33 +10,33 @@ KROWS = 106
 
 SCRATCH = {}
 for _dt, _bufs in (
-        ("int32", dict(raw=4, qi=4, tab=512, t16=16, t16b=16)),
-        ("float32", dict(par=4, msg1=4, ag=4, mask=128, dg=256, sq=2048, ysb=64)),
-        ("float16", dict(rhs=512, lm=256, big=384)),
+        ("int32", dict(raw=4, qi=4)),
+        ("float32", dict(ini=4, par=8, msg1=4, dg=256, sq=2048, ysb=64)),
+        ("float16", dict(rhs=512, lm=512)),
         ("uint16", dict(off=2048)),
-        ("bfloat16", dict(sel=16, cb=192, nfold=64, zb=128, xw=NS, xn=NS, xm=NS, xh=NS, gb0=8192, gb1=8192, gb2=8192,
-                          gb3=8192, out1=1024, land1=1024, clip=1024))):
+        ("bfloat16", dict(mask=128, idb=128, step=512, big=384, ab=8, zb=208, xw=NS, xn=NS, xm=NS, xh=NS,
+                          gb0=8192, gb1=8192, gb2=8192, gb3=8192, out1=1024, land1=1024, clip=1024))):
     for _k, _w in _bufs.items():
         SCRATCH[_k] = ("sbuf", [128, _w], _dt)
 for _k in ("pu", "pt", "pr0", "pr1", "po0", "po1", "po2", "py"):
     SCRATCH[_k] = ("psum", [128, 512], "float32")
-SEMAPHORES = ["sv", "ss", "sp", "sg", "ld", "ldx", "st", "sent", "m1", "xa", "xb", "hx", "hy", "l1a", "l1b"]
+SEMAPHORES = ["sv", "ss", "sp", "sg", "ld", "ld2", "ldx", "st", "sent", "m1", "xa", "xb", "hx", "hy", "l1a", "l1b"]
 
-JOBS = {"0a": (0, 0, 192, "pu", "pt"), "0b": (0, 192, 512, "pr0", "pr1"), "2": (2, 0, 512, "pu", "pt"),
-        "1a": (1, 0, 128, "pr0", "pr1"), "1b": (1, 128, 512, "po0", "po1"), "3": (3, 0, 512, "pu", "pt")}
+U_JOBS = {"0a": (0, 0, 128, "pu", None), "0b": (0, 128, 512, "po0", None), "2": (2, 0, 512, "pr0", None),
+          "3": (3, 0, 512, "pu", "0a"), "1": (1, 0, 512, "po0", "0b")}
+T_JOBS = {"0a": (0, 0, 128, "pt", None), "0b": (0, 128, 288, "po1", None), "0c": (0, 288, 512, "po2", None),
+          "2": (2, 0, 512, "pr1", None), "3": (3, 0, 512, "pt", "0a"), "1": (1, 0, 512, "po1", "0b")}
 
 V_ORDER = [
-    ("dg", 0), ("pre2",), ("conv", "0a"), ("pre3",), ("g", 0, 80, 144), ("conv", "0b"), ("lm", 2),
-    ("g", 0, 192, 280), ("g", 0, 344, 384), ("lm", 1), ("dg", 1), ("g", 0, 416, 464),
-    ("conv", "1a"), ("g", 1, 80, 120), ("conv", "1b"), ("lm", 3), ("g", 1, 200, 296), ("conv", "2"),
-    ("g", 1, 400, 512), ("g", 2, 104, 256), ("conv", "3"), ("g", 2, 392, 512),
-    ("g", 3, 136, 256), ("g", 3, 336, 456), ("g", 3, 456, 488), ("clip", 2), ("end",),
+    ("lm", 0), ("dg", 0), ("acopy",), ("pd",), ("pqs",), ("lm", 2), ("conv", "0a"), ("lm", 3), ("g", 0, 80, 128),
+    ("conv", "0b"), ("conv", "0c"), ("g", 0, 232, 312), ("lm", 1), ("dg", 1), ("conv", "2"), ("g", 0, 312, 416),
+    ("conv", "1"), ("g", 1, 128, 256), ("g", 1, 384, 512), ("conv", "3"), ("g", 2, 96, 352), ("g", 3, 96, 256),
+    ("g", 3, 360, 448), ("clip", 0), ("g", 3, 488, 512), ("clip", 1), ("clip", 2), ("end",),
 ]
 S_ORDER = [
-    ("sq", "0a"), ("sq", "0b"), ("g", 0, 0, 80), ("g", 0, 144, 192), ("sq", "2"), ("g", 0, 280, 344),
-    ("g", 0, 384, 416), ("sq", "1a"), ("sq", "1b"), ("g", 0, 464, 512), ("g", 1, 0, 80), ("g", 1, 120, 200),
-    ("g", 1, 296, 400), ("sq", "3"), ("ev", 1, 0), ("g", 2, 0, 104), ("ev", 1, 1), ("g", 2, 256, 392),
-    ("g", 3, 0, 136), ("g", 3, 256, 336), ("clip", 0), ("g", 3, 488, 512), ("clip", 1),
+    ("sq", "0a"), ("sq", "0b"), ("sq", "2"), ("g", 0, 0, 80), ("g", 0, 128, 232), ("sq", "1"), ("g", 0, 416, 512),
+    ("sq", "3"), ("g", 1, 0, 128), ("g", 1, 256, 384), ("ev", 0), ("g", 2, 0, 96), ("ev", 1), ("g", 2, 352, 512),
+    ("g", 3, 0, 96), ("g", 3, 256, 360), ("g", 3, 448, 488),
 ]
 
 
@@ -45,13 +45,12 @@ def pairs(b, lo, hi):
 
 
 P_ORDER = (
-    [("u", "0a"), ("a", 0), ("t", "0a"), ("add", "0a"), ("u", "0b"), ("t", "0b"), ("add", "0b"),
-     ("u", "2"), ("t", "2"),
-     ("a", 1), ("u", "1a"), ("t", "1a"), ("u", "1b"), ("add", "1a"), ("t", "1b"), ("add", "1b"), ("add", "2"),
-     ("u", "3")] + pairs(1, 0, 4) + [("t", "3")] + pairs(1, 4, 8) + [("add", "3"), ("open",)]
-    + pairs(0, 0, 8) + pairs(2, 0, 8) + pairs(3, 0, 4)
-    + [("land", 1, 0), ("land", 1, 1), ("land", 1, 2)] + pairs(3, 4, 7)
-    + [("sum", 0), ("r", 3, 7), ("sum", 2), ("sum", 1)]
+    [("big8", "0a"), ("big8", "0b"), ("half", "0a"), ("a",), ("half", "0b"), ("big8", "2"), ("u", "0a"), ("u", "0b"),
+     ("t", "0a"), ("u", "2"), ("t", "0b"), ("half", "0c"), ("t", "0c"), ("half", "2"), ("t", "2"), ("big8", "1"),
+     ("half", "1"), ("u", "1"), ("big8", "3"), ("u", "3"), ("t", "1"), ("half", "3"), ("t", "3"), ("open",)]
+    + pairs(0, 0, 2) + pairs(1, 0, 4) + pairs(0, 2, 6) + pairs(1, 4, 8) + pairs(0, 6, 8) + pairs(2, 0, 8)
+    + pairs(3, 0, 2) + [("land", 0), ("land", 1), ("land", 2)] + pairs(3, 2, 7)
+    + [("sum", 0), ("r", 3, 7), ("sum", 1), ("sum", 2)]
 )
 OWN = [("po0", 0, 4), ("po1", 4, 7), ("po2", 7, 8)]
 
@@ -88,8 +87,8 @@ def hand_on(g, core, T, topo):
             steps = [(("hx", k), T.xn, "xa", CA, NS, one), (("hy", k), T.xn, "xa", C1, CA, one),
                      (None, T.xm, "xb", E1, NS, two)]
         elif core == port:
-            steps = [(("hx", len(near_engines(r, core, T, topo))), T.xh, "hx", E0, EM, last),
-                     (None, T.xh, "hy", EM, E1, last)]
+            k = len(near_engines(r, core, T, topo))
+            steps = [(("hx", k), T.xh, "hx", E0, EM, last), (("hy", k), T.xh, "hy", EM, E1, last)]
         elif core == last:
             k = len(topo.engines(port, core))
             steps = [(("hx", k), T.xm, "xb", E0, EM, two), (("hy", k), T.xm, "xb", EM, E1, two)]
@@ -118,27 +117,13 @@ def rank_program(g, core, T, topo):
     A = AluOpType
     F = ActivationFunctionType
     q = rank
-    queues = {"v": g.vector, "s": g.scalar, "p": g.tensor, "g": g, "y": g.sync}
-    counts = {"sv": 0, "ss": 0, "sp": 0, "sg": 0}
+    v, s, p = g.vector, g.scalar, g.tensor
+    queues = {"v": v, "s": s, "p": p, "g": g, "y": g.sync}
     own_sem = {"v": "sv", "s": "ss", "p": "sp", "g": "sg"}
-    seen = {}
-    done = {}
+    work = {"v": [], "s": [], "p": [], "g": []}
 
-    def wait(qn, deps):
-        need = {}
-        for d in deps:
-            s, c = done[d] if d in done else d
-            need[s] = max(need.get(s, 0), c)
-        for s, c in need.items():
-            if seen.get((qn, s), 0) < c:
-                queues[qn].wait_ge(sem[s], c)
-                seen[(qn, s)] = c
-
-    def mark(qn, ins, key):
-        s = own_sem[qn]
-        ins.then_inc(sem[s], 1)
-        counts[s] += 1
-        assert done[key] == (s, counts[s]), key
+    def put(qn, key, deps, make):
+        work[qn].append((key, deps, make))
 
     def far_engines(src, dst):
         return topo.engines(cores[src % n], cores[dst % n])
@@ -147,189 +132,151 @@ def rank_program(g, core, T, topo):
     arr["xa"] = ("xa", len(far_engines(q + 1, q)) + 2 * len(topo.engines(helpers_of(q + 1, T, topo)[0], core)))
     other2, _, last2 = helpers_of(q + 2, T, topo)
     arr["xb"] = ("xb", len(far_engines(q + 2, q)) + len(topo.engines(other2, core)) + 2 * len(topo.engines(last2, core)))
-    LD, LDX = ("ld", 7 * 16), ("ldx", 8 * 16)
-
-    v_keys = ["mask1", "cb1", "qi1", "ag0", "ag1", "ag2", "ag3", "ag8", "par0", "ag4", "ag5", "ag6", "ag9", "ag10",
-              "ag7", "tabn", "big", "up", "rhs", "qa", "qb", "pd", "pq", ("lm", 0), "pa", "pq2", "down", "half"]
-    for o in V_ORDER:
-        v_keys += {"pre2": ["nfold1", "zb"], "pre3": ["t16b", "sel"]}.get(o[0], [o])
-    g_keys = ["tab", "maskd", "maskq", "maskp", "idb", "t16", "f0", "f1", "nf0", "nf1"]
-    for name, keys in (("sv", v_keys), ("ss", S_ORDER), ("sp", P_ORDER), ("sg", g_keys)):
-        for i, k in enumerate(keys):
-            done[k] = (name, i + 1)
+    LD, LD2, LDX = ("ld", 4 * 16), ("ld2", 3 * 16), ("ldx", 8 * 16)
 
     def gathers(b, lo, hi):
         return [o for o in V_ORDER + S_ORDER if o[0] == "g" and o[1] == b and o[2] < hi and o[3] > lo]
 
-    def job_of(b, lo, hi):
-        return [j for j, w in JOBS.items() if w[0] == b and w[1] < hi and w[2] > lo]
+    def job_of(jobs, b, lo, hi):
+        return [j for j, w in jobs.items() if w[0] == b and w[1] < hi and w[2] > lo]
 
-    for qn, ds, rows, chans in (("y", (0, 1), (64, 72), range(0, 4)), ("s", (2, 3), (96,), range(4, 8))):
-        e = queues[qn]
-        for r0 in rows:
-            e.dma_start(T.raw[r0:r0 + 8, 0:2], T.pa[:, :]).then_inc(sem.ld, 16)
-        for j in ds:
-            d = (q + j) % n
-            e.dma_start(T.raw[0:64, j:j + 1], T.de[:, 8 * d:8 * d + 8]).then_inc(sem.ld, 16)
+    def load_pa(e, r0):
+        e.dma_start(T.raw[r0:r0 + 8, 0:2], T.pa[:, :]).then_inc(sem.ld, 16)
+
+    def load_de(e, j, name):
+        d = (q + (0, 2, 1, 3)[j]) % n
+        e.dma_start(T.raw[0:64, j:j + 1], T.de[:, 8 * d:8 * d + 8]).then_inc(sem[name], 16)
+
+    def load_x(e, chans):
         for c in chans:
             e.dma_start(T.xw[16 * c:16 * c + 16, :], T.x[:, NS * c:NS * (c + 1)]).then_inc(sem.ldx, 16)
 
+    load_de(g.sync, 0, "ld")
+    load_pa(s, 64)
+    load_pa(g.sync, 96)
+    load_pa(s, 72)
+    load_de(g.sync, 3, "ld2")
+    load_de(s, 2, "ld2")
+    load_de(s, 1, "ld2")
+    load_x(g.sync, range(0, 4))
+    load_x(s, range(4, 8))
+
     sent = [0]
 
-    def send(out_ap, in_ap, name, to):
-        eng = far_engines(q, to)
-        rid, pid, _ = topo.addr(cores[to % n])
-        g.remote_dma(out_ap, in_ap, sem[name], sem.sent, pid, rid, bits(eng))
+    def send(key, deps, out_ap, in_ap, name, to, eng):
+        rid, pid, _ = topo.addr(to)
         sent[0] += len(eng)
+        put("g", key, deps, lambda: g.remote_dma(out_ap, in_ap, sem[name], sem.sent, pid, rid, bits(eng)))
 
-    def copy_to(helper, name, lo, hi):
-        eng = near_engines(q, helper, T, topo)
-        rid, pid, _ = topo.addr(helper)
-        g.remote_dma(T.xh[:, lo:hi], T.xw[:, lo:hi], sem[name], sem.sent, pid, rid, bits(eng))
-        sent[0] += len(eng)
+    def far(deps, out_ap, in_ap, name, to):
+        send(None, deps, out_ap, in_ap, name, cores[to % n], far_engines(q, to))
 
-    def gop(key, deps, make):
-        wait("g", deps + [("sg", counts["sg"])])
-        mark("g", make(), key)
+    def near(deps, helper, name, lo, hi):
+        send(None, deps, T.xh[:, lo:hi], T.xw[:, lo:hi], name, helper, near_engines(q, helper, T, topo))
 
     def pick(key, deps, view, pat):
-        gop(key, deps, lambda: g.affine_select(view, view, pat, A.is_equal, 0.0, 0, 1))
+        put("g", key, deps, lambda: g.affine_select(view, view, pat, A.is_equal, 0.0, 0, 1))
 
-    gop("tab", [], lambda: g.iota(T.tab[:], [[1, 512]], 0, 0))
+    def mark_ones(key, deps, view, base):
+        put("g", key, deps, lambda: g.affine_select(view, view, [[-1, view.shape[1]]], A.not_equal, 1.0, base, 1))
+
     pick("maskd", ["mask1"], T.mask[0:64, :], [[-1, 8], [0, 2], [-8, 8]])
     pick("maskq", [], T.mask[64:96, :], [[0, 8], [-8, 2], [-1, 8]])
     pick("maskp", [], T.mask[96:104, :], [[0, 16], [-1, 8]])
-    pick("idb", ["cb1"], T.cb[:, 0:128], [[-1, 128]])
-    wait("g", ["pq2"])
-    send(T.msg1[:], T.par[:], "m1", q - 1)
-    gop("t16", [], lambda: g.iota(T.t16[:], [[-1, 16]], 16, 1))
+    pick("idb", ["idb1", "maskp"], T.idb[:], [[-1, 128]])
+    far([("pqs",)], T.msg1[:, 0:2], T.par[:, 3:5], "m1", q - 1)
     other, port, _ = helpers_of(q, T, topo)
-    wait("g", [LDX])
-    copy_to(other, "hx", CA, NS)
-    send(T.xn[:, 0:C1], T.xw[:, 0:C1], "xa", q - 1)
-    copy_to(other, "hy", E1, CA)
-    copy_to(port, "hx", E0, E1)
-    send(T.xm[:, 0:E0], T.xw[:, 0:E0], "xb", q - 2)
-    for key, view in (("f0", T.cb[0:64, 128:192]), ("f1", T.cb[64:128, 128:192]),
-                      ("nf0", T.nfold[0:64, :]), ("nf1", T.nfold[64:128, :])):
-        pick(key, ["nfold1"], view, [[-1, 64]])
+    near([LDX], port, "hx", E0, EM)
+    far([], T.xn[:, 0:C1], T.xw[:, 0:C1], "xa", q - 1)
+    near([], other, "hx", CA, NS)
+    near([], port, "hy", EM, E1)
+    near([], other, "hy", E1, CA)
+    far([], T.xm[:, 0:E0], T.xw[:, 0:E0], "xb", q - 2)
+    zeros, sel, fold = T.zb[:, 0:128], T.zb[:, 128:144], T.zb[:, 144:208]
+    put("g", "zb", ["idb"], lambda: g.iota(T.zb[:], [[0, 208]], 0, 0, allow_small_or_imprecise_dtypes=True))
+    for c in range(8):
+        mark_ones(("sel", c), ["zb"] if c == 0 else [("sel", c - 1)], sel, -16 * c)
     for k in range(2):
-        wait("g", [("ev", 1, k)])
-        send(T.land1[:, 512 * k:512 * k + 512], T.out1[:, 512 * k:512 * k + 512], "l1" + "ab"[k], q + 1)
+        mark_ones(("fold", k), [("fold", 0)] if k else [("sel", 7)], fold, -64 * k)
+    for k in range(2):
+        far([("ev", k)], T.land1[:, 512 * k:512 * k + 512], T.out1[:, 512 * k:512 * k + 512], "l1" + "ab"[k], q + 1)
 
-    v = g.vector
+    for key, deps, view, val in (
+            ("mask1", [], T.mask[:], 1.0), ("step0", [], T.step[:], 0.0),
+            ("ini0", [], T.ini[0:64, 0:1], 1.0), ("ini1", [], T.ini[64:96, 0:1], -1.0 / 256),
+            ("ini2", [], T.ini[96:128, 0:1], 3.5), ("idb1", [], T.idb[:], 1.0),
+            ("step1", ["step0"], T.step[64:96, :], 1.0 / 256), ("step2", [], T.step[96:104, 32::32], 1.0 / 512),
+            ("ini3", ["ini2"], T.ini[64:72, 0:1], -2.0 / 256), ("ini4", [], T.ini[96:105, 0:1], -2047.0 / 512),
+            ("qi1", [], T.qi[64:128, 0:1], 1), ("ini5", ["ini4"], T.ini[96:104, 0:1], 0.0)):
+        put("v", key, deps, lambda view=view, val=val: v.memset(view, val))
+    put("v", "rhs", ["ini5"], lambda: v.tensor_tensor_scan(T.rhs[:], T.step[:], T.step[:], T.ini[:, 0:1], A.add, A.add))
+    for key, deps, view, val in (
+            ("half0", ["step1"], T.big[64:66, 256:384], 1.0 / 32), ("big8", [], T.big[64:65, 0:128], 256 * BIG8),
+            ("half1", ["half0"], T.big[64:65, 256:384], -128.0), ("big1", [], T.big[64:65, 128:256], 256 * BIG1)):
+        put("s", key, deps, lambda view=view, val=val: s.activation(
+            view, T.step[64:64 + view.shape[0], 0:128], F.Identity, bias=val, scale=0.0))
 
-    def vop(key, deps, make):
-        wait("v", deps)
-        mark("v", make(), key)
+    def delays(lo, hi):
+        return v.tensor_scalar(T.par[0:64, lo:hi], T.raw[0:64, lo:hi], float(-CENTER), None, A.add)
 
-    for key, view, val in (
-            ("mask1", T.mask[:], 1.0), ("cb1", T.cb[:], 1.0), ("qi1", T.qi[64:128, :], 1),
-            ("ag0", T.ag[:, 0:1], 0.0), ("ag1", T.ag[0:64, 1:2], 2048.0), ("ag2", T.ag[64:96, 1:2], 1.0 / 256),
-            ("ag3", T.ag[96:128, 1:2], 3.5), ("ag8", T.ag[64:KROWS, 2:3], -585.0 / 4096),
-            ("par0", T.par[64:128, :], 0.0),
-            ("ag4", T.ag[64:80, 0:1], 2.0 / 256), ("ag5", T.ag[96:104, 0:1], 1.0 / 256),
-            ("ag6", T.ag[64:72, 1:2], 0.0), ("ag9", T.ag[96:105, 1:2], -2047.0 / 512),
-            ("ag10", T.ag[64:105, 2:3], 0.0), ("ag7", T.ag[96:104, 1:2], 0.0)):
-        vop(key, {"ag4": ["ag8"], "ag7": ["ag9"]}.get(key, []), lambda: v.memset(view, val))
+    put("v", "qa", [LD, "qi1"], lambda: v.tensor_scalar(T.qi[64:80, 0:1], T.raw[64:80, 0:1], 6, None, A.arith_shift_right))
+    put("v", "qb", [], lambda: v.tensor_scalar(T.qi[96:104, 0:1], T.raw[96:104, 0:1], 63, None, A.bitwise_and))
+    put("v", "pa", [], lambda: v.tensor_scalar(T.ab[64:80, 0:1], T.raw[64:80, 1:2], 1.0 / 4096, None, A.mult))
+    put("v", "pd", [], lambda: delays(0, 1))
+    put("v", "pq", ["qb"], lambda: v.tensor_copy(T.par[64:128, 0:1], T.qi[64:128, 0:1]))
 
-    def row(key, i, val):
-        vop(key, [], lambda: v.tensor_scalar(T.big[0:1, 128 * i:128 * i + 128], T.tab[0:1, 0:128], 0.0, val / 2048,
-                                             A.mult, A.add))
-
-    vop("tabn", ["tab"], lambda: v.tensor_scalar(T.tab[96:128, :], T.tab[96:128, :], 5, None, A.arith_shift_right))
-    row("big", 0, BIG8)
-    row("up", 1, BIG1)
-    vop("rhs", ["tabn"], lambda: v.tensor_scalar(T.rhs[:], T.tab[:], T.ag[:, 0:1], T.ag[:, 1:2], A.mult, A.add))
-    vop("qa", [LD], lambda: v.tensor_scalar(T.qi[64:80, 0:1], T.raw[64:80, 0:1], 6, None, A.arith_shift_right))
-    vop("qb", [], lambda: v.tensor_scalar(T.qi[96:104, 0:1], T.raw[96:104, 0:1], 63, None, A.bitwise_and))
-    vop("pd", [], lambda: v.tensor_scalar(T.par[0:64, :], T.raw[0:64, :], float(-CENTER), 1.0 / 2048, A.add, A.mult))
-    vop("pq", ["qb"], lambda: v.tensor_copy(T.par[64:128, 0:1], T.qi[64:128, 0:1]))
-
-    src_of = {0: T.par, 1: T.msg1, 2: T.par, 3: T.par}
-    col_of = {0: 0, 1: n - 1, 2: 1, 3: 2}
-    slot_of = {0: 0, 1: 1, 2: 0, 3: 0}
-
-    def lm(b):
-        c, s0, rows = col_of[b], 128 * slot_of[b], 64 if b >= 2 else KROWS
-        return v.tensor_scalar(T.lm[0:rows, s0:s0 + 128], T.mask[0:rows, :], src_of[b][0:rows, c:c + 1], None, A.mult)
-
-    vop(("lm", 0), ["pq", "maskp"], lambda: lm(0))
-    vop("pa", [], lambda: v.tensor_scalar(T.par[96:104, 1:2], T.raw[96:104, 1:2], 1.0 / 4096, None, A.mult))
-    vop("pq2", [], lambda: v.tensor_copy(T.par[64:128, 3:4], T.qi[64:128, 0:1]))
-    row("down", 2, -BIG1)
-    vop("half", [], lambda: v.tensor_scalar(T.big[64:KROWS, 0:128], T.tab[64:KROWS, 0:128], 0.0, T.ag[64:KROWS, 2:3],
-                                            A.mult, A.add))
-
-    def gather_deps(o):
-        b = o[1]
-        return [("conv", j) for j in job_of(b, o[2], o[3])] + [{2: arr["xa"], 3: arr["xb"]}.get(b, LDX)]
-
-    def operand(o):
-        b = o[1]
-        win = {2: T.xn, 3: T.xm}.get(b, T.xw)
-        return T["gb%d" % b][:, 16 * o[2]:16 * o[3]], win[:, 0:NS].indirect(T.off[:, 512 * b + o[2]:512 * b + o[3]])
+    numbers = {0: T.par[0:KROWS, 0:1], 1: T.msg1[0:KROWS, 0:1], 2: T.par[0:KROWS, 2:3], 3: T.par[0:KROWS, 1:2]}
+    accel = {0: T.py[:, 64:65], 1: T.msg1[:, 1:2]}
+    lm_deps = {0: ["pq", "maskp"], 1: [arr["m1"]], 2: [("pqs",)], 3: [("pqs",)]}
 
     def own_done(k):
-        return pairs(3, OWN[k][1], OWN[k][2]) + [("land", 1, k)]
+        return pairs(3, OWN[k][1], OWN[k][2]) + [("land", k)]
 
-    scalar_clipped = sum(2 * (OWN[o[1]][2] - OWN[o[1]][1]) for o in S_ORDER if o[0] == "clip")
-
-    for o in V_ORDER:
+    def elementwise(qn, o):
         kind = o[0]
-        if kind == "pre2":
-            vop("nfold1", [], lambda: v.memset(T.nfold[:], -1.0))
-            vop("zb", [], lambda: v.memset(T.zb[:], 0.0))
-        elif kind == "pre3":
-            vop("t16b", ["t16"], lambda: v.tensor_scalar(T.t16b[:], T.t16[:], 15, None, A.bitwise_and))
-            vop("sel", ["t16b"], lambda: v.tensor_scalar(T.sel[:], T.t16b[:], 0.0, None, A.is_equal))
-        elif kind == "lm":
+        if kind == "lm":
             b = o[1]
-            vop(o, {1: [arr["m1"]], 2: [("t", "0a"), ("t", "0b")], 3: [("t", "2")]}[b], lambda: lm(b))
+            put(qn, o, lm_deps[b], lambda: v.tensor_scalar(
+                T.lm[0:KROWS, 128 * b:128 * b + 128], T.mask[0:KROWS, :], numbers[b], None, A.mult))
+        elif kind == "pd":
+            put(qn, o, [LD2], lambda: delays(1, 4))
+        elif kind == "acopy":
+            put(qn, o, [("a",)], lambda: v.tensor_copy(T.par[:, 4:5], T.py[:, 64:65]))
+        elif kind == "pqs":
+            put(qn, o, ["pq"], lambda: v.tensor_scalar(
+                T.par[64:128, 1:4], T.step[64:128, 0:3], 0.0, T.par[64:128, 0:1], A.mult, A.add))
         elif kind == "dg":
             b = o[1]
-            vop(o, [("a", b), "idb"], lambda: v.tensor_scalar(
-                T.dg[:, 128 * b:128 * b + 128], T.cb[:, 0:128], T.py[:, 64 + b:65 + b], None, A.mult))
+            put(qn, o, ["idb", arr["m1"] if b else ("a",)], lambda: v.tensor_scalar(
+                T.dg[:, 128 * b:128 * b + 128], T.idb[:], accel[b], None, A.mult))
+        elif kind == "sq":
+            b, lo, hi, bu = U_JOBS[o[1]][:4]
+            put(qn, o, [("u", o[1])], lambda: s.activation(
+                T.sq[:, 512 * b + lo:512 * b + hi], T[bu][:, lo:hi], F.Square, bias=CENTER / 8 - BIG8 / 8, scale=0.125))
         elif kind == "conv":
-            b, lo, hi, bu, bt = JOBS[o[1]]
-            vop(o, [("add", o[1])], lambda: v.tensor_scalar(
-                T.off[:, 512 * b + lo:512 * b + hi], T[bt][:, lo:hi], BIG1, CENTER - BIG1, A.add, A.add))
+            b, lo, hi, bt = T_JOBS[o[1]][:4]
+            put(qn, o, [("t", o[1])], lambda: v.tensor_scalar(
+                T.off[:, 512 * b + lo:512 * b + hi], T[bt][:, lo:hi], CENTER - BIG1, None, A.add))
         elif kind == "g":
-            out, src = operand(o)
-            vop(o, gather_deps(o), lambda: v.tensor_copy(out, src))
+            b, lo, hi = o[1:]
+            out = T["gb%d" % b][:, 16 * lo:16 * hi]
+            src = {2: T.xn, 3: T.xm}.get(b, T.xw)[:, 0:NS].indirect(T.off[:, 512 * b + lo:512 * b + hi])
+            put(qn, o, [("conv", j) for j in job_of(T_JOBS, b, lo, hi)] + [{2: arr["xa"], 3: arr["xb"]}.get(b, LDX)],
+                (lambda: v.tensor_copy(out, src)) if qn == "v" else (lambda: s.activation(out, src, F.Copy)))
+        elif kind == "ev":
+            k = o[1]
+            put(qn, o, pairs(1, 4 * k, 4 * k + 4), lambda: s.activation(
+                T.out1[:, 512 * k:512 * k + 512], T["pr%d" % k][:], F.Copy))
         elif kind == "clip":
             bank, lo, hi = OWN[o[1]]
-            vop(o, own_done(o[1]), lambda: v.tensor_scalar(
+            put(qn, o, own_done(o[1]), lambda: v.tensor_scalar(
                 T.clip[:, 128 * lo:128 * hi], T[bank][:, 0:128 * (hi - lo)], 255.0, None, A.min))
         elif kind == "end":
-            vop(o, [("sum", 0), ("sum", 1), ("sum", 2)], lambda: v.tensor_scalar(
-                T.ysb[:], T.py[:, 0:64], 255.0 * scalar_clipped, None, A.add))
+            put(qn, o, [("sum", k) for k in range(len(OWN))], lambda: v.tensor_copy(T.ysb[:], T.py[:, 0:64]))
 
-    s = g.scalar
-    for o in S_ORDER:
-        kind = o[0]
-        if kind == "sq":
-            b, lo, hi, bu, bt = JOBS[o[1]]
-            wait("s", [("u", o[1])])
-            mark("s", s.activation(T.sq[:, 512 * b + lo:512 * b + hi], T[bu][:, lo:hi], F.Square,
-                                   bias=CENTER / 8 - BIG8 / 8, scale=0.125), o)
-        elif kind == "g":
-            out, src = operand(o)
-            wait("s", gather_deps(o))
-            mark("s", s.activation(out, src, F.Copy), o)
-        elif kind == "ev":
-            k = o[2]
-            wait("s", pairs(1, 4 * k, 4 * k + 4))
-            mark("s", s.activation(T.out1[:, 512 * k:512 * k + 512], T["pr%d" % k][:], F.Copy), o)
-        elif kind == "clip":
-            bank, lo, hi = OWN[o[1]]
-            wait("s", own_done(o[1]))
-            mark("s", s.activation(T.clip[:, 128 * lo:128 * hi], T[bank][:, 0:128 * (hi - lo)], F.Relu,
-                                   bias=255.0, scale=-1.0), o)
-
-    p = g.tensor
-    bank_free = {"0a": [], "0b": [], "2": [("sq", "0a"), ("conv", "0a")], "1a": [("sq", "0b"), ("conv", "0b")],
-                 "1b": [], "3": [("sq", "2"), ("conv", "2")]}
+    for qn, order in (("v", V_ORDER), ("s", S_ORDER)):
+        for o in order:
+            elementwise(qn, o)
 
     def own_bank(m):
         return [k for k, w in enumerate(OWN) if w[1] <= m < w[2]][0]
@@ -339,69 +286,102 @@ def rank_program(g, core, T, topo):
         if o[0] == "r" and o[1] == 3:
             last_own[own_bank(o[2])] = o
         elif o[0] == "land":
-            last_own[o[2]] = o
+            last_own[o[1]] = o
     sums = [o for o in P_ORDER if o[0] == "sum"]
-    for o in P_ORDER:
+
+    def constant(bank, lo, hi, i, rows, start):
+        return p.matmul(T[bank][:, lo:hi], T.big[64:64 + rows, 128 * i:128 * i + 128], T.step[64:64 + rows, lo:hi],
+                        start, False)
+
+    def times(bank, b, lo, hi, rows):
+        return p.matmul(T[bank][:, lo:hi], T.lm[0:rows, 128 * b:128 * b + 128], T.rhs[0:rows, lo:hi], False, True)
+
+    def tensor(o):
         kind = o[0]
+        if kind in ("big8", "half", "u", "t"):
+            b, lo, hi, bu, before = (U_JOBS if kind in ("big8", "u") else T_JOBS)[o[1]]
+            bt, s0 = bu, 128 * (b == 1)
         if kind == "a":
-            b = o[1]
-            wait("p", {0: ["pa"], 1: [arr["m1"], ("dg", 0)]}[b])
-            ins = p.matmul(T.py[:, 64 + b:65 + b], T.mask[64:104, :], src_of[b][64:104, 1:2], True, True)
+            put("p", o, ["pa", "maskq"], lambda: p.matmul(T.py[:, 64:65], T.mask[64:80, :], T.ab[64:80, 0:1], True, True))
+        elif kind == "big8":
+            put("p", o, ["big8"] + ([("sq", before)] if before else []), lambda: constant(bu, lo, hi, 0, 1, True))
+        elif kind == "half":
+            put("p", o, ["half1"] + ([("conv", before)] if before else []), lambda: constant(bt, lo, hi, 2, 2, True))
         elif kind == "u":
-            b, lo, hi, bu, bt = JOBS[o[1]]
-            s0 = 128 * slot_of[b]
-            wait("p", [("lm", b)] + bank_free[o[1]])
-            p.matmul(T[bu][:, lo:hi], T.lm[0:KROWS - 1, s0:s0 + 128], T.rhs[0:KROWS - 1, lo:hi], True, False)
-            ins = p.matmul(T[bu][:, lo:hi], T.big[0:1, 0:128], T.rhs[0:1, lo:hi], False, True)
+            put("p", o, [("lm", b), "rhs"], lambda: times(bu, b, lo, hi, KROWS - 1))
         elif kind == "t":
-            b, lo, hi, bu, bt = JOBS[o[1]]
-            s0 = 128 * slot_of[b]
-            wait("p", [("lm", b), "half"] + bank_free[o[1]])
-            p.matmul(T[bt][:, lo:hi], T.lm[0:KROWS, s0:s0 + 128], T.rhs[0:KROWS, lo:hi], True, False)
-            p.matmul(T[bt][:, lo:hi], T.big[0:1, 128:256], T.rhs[0:1, lo:hi], False, False)
-            p.matmul(T[bt][:, lo:hi], T.big[0:1, 256:384], T.rhs[0:1, lo:hi], False, False)
-            ins = p.matmul(T[bt][:, lo:hi], T.big[64:KROWS, 0:128], T.rhs[64:KROWS, lo:hi], False, False)
-        elif kind == "add":
-            b, lo, hi, bu, bt = JOBS[o[1]]
-            s0 = 128 * slot_of[b]
-            wait("p", [("sq", o[1]), ("dg", slot_of[b])])
-            ins = p.matmul(T[bt][:, lo:hi], T.dg[:, s0:s0 + 128], T.sq[:, 512 * b + lo:512 * b + hi], False, True)
+            def place():
+                p.matmul(T[bt][:, lo:hi], T.dg[:, s0:s0 + 128], T.sq[:, 512 * b + lo:512 * b + hi], False, False)
+                constant(bt, lo, hi, 1, 1, False)
+                return times(bt, b, lo, hi, KROWS)
+            put("p", o, [("sq", j) for j in job_of(U_JOBS, b, lo, hi)] + [("dg", int(b == 1)), "big1"], place)
         elif kind == "open":
-            wait("p", gathers(0, 0, 32) + ["zb", ("sq", "1b"), ("conv", "1b")])
-            for bank, lo, hi in OWN:
-                ins = p.matmul(T[bank][:, 0:128 * (hi - lo)], T.zb[:], T.gb0[:, 0:128 * (hi - lo)], True, False)
+            def zero():
+                for bank, lo, hi in OWN:
+                    ins = p.matmul(T[bank][:, 0:128 * (hi - lo)], zeros, T.gb0[:, 0:128 * (hi - lo)], True, False)
+                return ins
+            put("p", o, gathers(0, 0, 32) + ["zb", ("sq", "1"), ("conv", "1"), ("conv", "0c")], zero)
         elif kind == "r":
             b, m = o[1], o[2]
-            deps = gathers(b, 64 * m, 64 * m + 64) + ["sel"]
+            deps = gathers(b, 64 * m, 64 * m + 64) + [("sel", 7)]
             alone = b == 1
             if alone:
                 bank, c0, final = "pr%d" % (m // 4), 128 * (m % 4), False
-                deps += [("sq", "1a"), ("conv", "1a")]
+                deps += [("sq", "2"), ("conv", "2")]
             else:
                 k = own_bank(m)
                 bank, c0, final = OWN[k][0], 128 * (m - OWN[k][1]), last_own[k] == o
-            wait("p", deps)
-            for t in range(8):
-                ins = p.matmul(T[bank][:, c0 + 16 * t:c0 + 16 * t + 16],
-                               T["gb%d" % b][:, 1024 * m + t:1024 * m + 1024:8], T.sel[:],
-                               alone, alone or (final and t == 7))
+
+            def channels():
+                for t in range(8):
+                    ins = p.matmul(T[bank][:, c0 + 16 * t:c0 + 16 * t + 16],
+                                   T["gb%d" % b][:, 1024 * m + t:1024 * m + 1024:8], sel,
+                                   alone, alone or (final and t == 7))
+                return ins
+            put("p", o, deps, channels)
         elif kind == "land":
-            k = o[2]
+            k = o[1]
             bank, lo, hi = OWN[k]
-            wait("p", [arr["l1a" if k == 0 else "l1b"], "idb"])
-            ins = p.matmul(T[bank][:, 0:128 * (hi - lo)], T.cb[:, 0:128], T.land1[:, 128 * lo:128 * hi],
-                           False, last_own[k] == o)
+            put("p", o, [arr["l1a" if k == 0 else "l1b"], "idb"], lambda: p.matmul(
+                T[bank][:, 0:128 * (hi - lo)], T.idb[:], T.land1[:, 128 * lo:128 * hi], False, last_own[k] == o))
         elif kind == "sum":
             k = o[1]
             bank, lo, hi = OWN[k]
-            wait("p", [("clip", k), ("dg", 1), "nf1"])
-            fold = T.nfold[:] if ("clip", k) in S_ORDER else T.cb[:, 128:192]
-            for m in range(lo, hi):
-                ins = p.matmul(T.py[:, 0:64], T.clip[:, 128 * m:128 * m + 128], fold,
-                               o == sums[0] and m == lo, o == sums[-1] and m == hi - 1)
-        mark("p", ins, o)
+
+            def pulses():
+                for m in range(lo, hi):
+                    ins = p.matmul(T.py[:, 0:64], T.clip[:, 128 * m:128 * m + 128], fold,
+                                   o == sums[0] and m == lo, o == sums[-1] and m == hi - 1)
+                return ins
+            put("p", o, [("clip", k), ("acopy",), ("fold", 1)], pulses)
+
+    for o in P_ORDER:
+        tensor(o)
+
+    done = {}
+    for qn, items in work.items():
+        for i, key in enumerate([w[0] for w in items if w[0] is not None]):
+            done[key] = (own_sem[qn], i + 1)
+    seen = {}
+
+    def wait(qn, deps):
+        need = {}
+        for d in deps:
+            name, c = done[d] if d in done else d
+            need[name] = max(need.get(name, 0), c)
+        for name, c in need.items():
+            if seen.get((qn, name), 0) < c:
+                queues[qn].wait_ge(sem[name], c)
+                seen[(qn, name)] = c
+
+    for qn, items in work.items():
+        for key, deps, make in items:
+            wait(qn, deps)
+            ins = make()
+            if key is not None:
+                ins.then_inc(sem[own_sem[qn]], 1)
 
     wait("y", [("end",)])
     g.sync.dma_start(T.y[:, :], T.ysb[:]).then_inc(sem.st, 16)
     g.sync.wait_ge(sem.st, 16)
-    wait("g", [("sent", sent[0]), ("sg", counts["sg"]), ("ss", counts["ss"]), ("sp", counts["sp"])])
+    wait("g", [("sent", sent[0])] + [(own_sem[qn], sum(w[0] is not None for w in work[qn])) for qn in "gsp"])

@@ -2,7 +2,9 @@ from concourse.mybir import AluOpType, ActivationFunctionType
 
 SIM_CORES = 64
 NS = 2560
-C1, CA, E0, EM, E1 = 1664, 2112, 896, 1216, 1536
+C1, C2, E0, EM, E1 = 1856, 1280, 768, 1280, 1792
+XA = C1
+SENDS = ["other,0", "far,1", "port,0", "other,1", "far,2", "port,1", "far,3"]
 CENTER = 1280
 BIG8 = 1.5 * 2.0 ** 26
 BIG1 = 1.5 * 2.0 ** 23
@@ -11,48 +13,46 @@ KROWS = 106
 SCRATCH = {}
 for _dt, _bufs in (
         ("int32", dict(raw=4, qi=4)),
-        ("float32", dict(ini=4, par=8, msg1=4, dg=256, sq=2048, ysb=64)),
+        ("float32", dict(ini=4, par=4, dg=128, sq=2048, ysb=64)),
         ("float16", dict(rhs=512, lm=512)),
         ("uint16", dict(off=2048)),
-        ("bfloat16", dict(mask=128, idb=128, step=512, big=384, ab=8, zb=208, xw=NS, xn=NS, xm=NS, xh=NS,
-                          gb0=8192, gb1=8192, gb2=8192, gb3=8192, out1=1024, land1=1024, clip=1024))):
+        ("bfloat16", dict(mask=128, idb=128, step=512, big=512, ab=8, f64=64, f32=32, f16=16, x0=NS, x1=NS, x2=NS, x3=NS,
+                          gb0=8192, gb1=8192, gb2=8192, gb3=8192, clip=1024))):
     for _k, _w in _bufs.items():
         SCRATCH[_k] = ("sbuf", [128, _w], _dt)
-for _k in ("pu", "pt", "pr0", "pr1", "po0", "po1", "po2", "py"):
+for _k in ("pu", "pt", "pv", "pw", "po0", "po1", "po2", "py"):
     SCRATCH[_k] = ("psum", [128, 512], "float32")
-SEMAPHORES = ["sv", "ss", "sp", "sg", "ld", "ld2", "ldx", "st", "sent", "m1", "xa", "xb", "hx", "hy", "l1a", "l1b"]
+SEMAPHORES = ["sv", "ss", "sp", "sg", "ld", "ld2", "ldx", "lda", "st", "sent", "a1", "a2", "a3", "hx", "hy"]
 
-U_JOBS = {"0a": (0, 0, 128, "pu", None), "0b": (0, 128, 512, "po0", None), "2": (2, 0, 512, "pr0", None),
-          "3": (3, 0, 512, "pu", "0a"), "1": (1, 0, 512, "po0", "0b")}
+U_JOBS = {"0a": (0, 0, 128, "pu", None), "0b": (0, 128, 512, "po0", None), "1a": (1, 0, 512, "pv", None),
+          "2a": (2, 0, 512, "pu", "0a"), "3a": (3, 0, 512, "pv", "1a")}
 T_JOBS = {"0a": (0, 0, 128, "pt", None), "0b": (0, 128, 288, "po1", None), "0c": (0, 288, 512, "po2", None),
-          "2": (2, 0, 512, "pr1", None), "3": (3, 0, 512, "pt", "0a"), "1": (1, 0, 512, "po1", "0b")}
-
-V_ORDER = [
-    ("lm", 0), ("dg", 0), ("acopy",), ("pd",), ("pqs",), ("lm", 2), ("conv", "0a"), ("lm", 3), ("g", 0, 80, 128),
-    ("conv", "0b"), ("conv", "0c"), ("g", 0, 232, 312), ("lm", 1), ("dg", 1), ("conv", "2"), ("g", 0, 312, 416),
-    ("conv", "1"), ("g", 1, 128, 256), ("g", 1, 384, 512), ("conv", "3"), ("g", 2, 96, 352), ("g", 3, 96, 256),
-    ("g", 3, 360, 448), ("clip", 0), ("g", 3, 488, 512), ("clip", 1), ("clip", 2), ("end",),
-]
-S_ORDER = [
-    ("sq", "0a"), ("sq", "0b"), ("sq", "2"), ("g", 0, 0, 80), ("g", 0, 128, 232), ("sq", "1"), ("g", 0, 416, 512),
-    ("sq", "3"), ("g", 1, 0, 128), ("g", 1, 256, 384), ("ev", 0), ("g", 2, 0, 96), ("ev", 1), ("g", 2, 352, 512),
-    ("g", 3, 0, 96), ("g", 3, 256, 360), ("g", 3, 448, 488),
-]
+          "1a": (1, 0, 512, "pw", None), "2a": (2, 0, 512, "pt", "0a"), "3a": (3, 0, 512, "pw", "1a")}
+EARLY = ("0a",)
+OWN = [("po0", 0, 4), ("po1", 4, 7), ("po2", 7, 8)]
 
 
 def pairs(b, lo, hi):
     return [("r", b, m) for m in range(lo, hi)]
 
 
-P_ORDER = (
-    [("big8", "0a"), ("big8", "0b"), ("half", "0a"), ("a",), ("half", "0b"), ("big8", "2"), ("u", "0a"), ("u", "0b"),
-     ("t", "0a"), ("u", "2"), ("t", "0b"), ("half", "0c"), ("t", "0c"), ("half", "2"), ("t", "2"), ("big8", "1"),
-     ("half", "1"), ("u", "1"), ("big8", "3"), ("u", "3"), ("t", "1"), ("half", "3"), ("t", "3"), ("open",)]
-    + pairs(0, 0, 2) + pairs(1, 0, 4) + pairs(0, 2, 6) + pairs(1, 4, 8) + pairs(0, 6, 8) + pairs(2, 0, 8)
-    + pairs(3, 0, 2) + [("land", 0), ("land", 1), ("land", 2)] + pairs(3, 2, 7)
-    + [("sum", 0), ("r", 3, 7), ("sum", 1), ("sum", 2)]
-)
-OWN = [("po0", 0, 4), ("po1", 4, 7), ("po2", 7, 8)]
+def steps(text):
+    out = []
+    for word in text.split():
+        o = tuple(int(x) if x.isdigit() else x for x in word.split(","))
+        out += pairs(*o[1:]) if o[0] == "r" else [o]
+    return out
+
+
+V_ORDER = steps("""lm,0 pd pqs dg fold,0 lm,1 fold,1 lm,2 lm,3 conv,0a g,0,64,112 conv,0b conv,0c fold,2 g,0,112,328
+    conv,1a conv,2a g,1,256,512 conv,3a g,2,256,512 g,3,0,128 g,3,368,448 g,3,448,484 clip,1 clip,2 end""")
+S_ORDER = steps("""sq,0a sq,0b sq,1a g,0,0,64 g,0,328,368 sq,2a sq,3a g,0,368,512 g,1,0,256 g,2,0,256
+    g,3,128,320 g,3,320,368 g,3,484,512 clip,0""")
+P_ORDER = steps("""big8,0a big8,0b big8,1a half,0a half,0b half,0c a u,0a u,0b z,0a t,0a u,1a t,0b t,0c half,1a
+    big8,2a big8,3a u,2a u,3a half,2a t,1a t,2a open half,3a r,0,0,4 t,3a r,0,4,8 r,1,0,8 r,2,0,8 r,3,0,8
+    sum,0 sum,1 sum,2""")
+LOADS = {"y": "de,0 pa,96 de,3 xa,0 xa,1 xa,2 xa,3 xa,4 xa,5 x,0 x,1 x,2 x,3 x,4 x,5",
+         "s": "pa,64 pa,72 de,1 de,2 xa,6 xa,7 x,6 x,7"}
 
 
 def bits(engines):
@@ -61,11 +61,11 @@ def bits(engines):
 
 def helpers_of(r, T, topo):
     cores = list(T.cores)
-    core, one, two = cores[r % len(cores)], cores[(r - 1) % len(cores)], cores[(r - 2) % len(cores)]
+    core = cores[r % len(cores)]
     free = [c for c in topo.cores_of(core) if T.rank_of(c) is None]
-    other = [c for c in free if topo.die(c) != topo.die(core) and topo.may_write(c, one) and topo.may_write(c, two)][0]
-    last = [c for c in range(SIM_CORES) if topo.mates(topo.chip(c), topo.chip(two)) and T.rank_of(c) is None
-            and topo.die(c) == topo.die(core) and topo.may_write(c, two)][0]
+    other = [c for c in free if topo.die(c) != topo.die(core)][0]
+    last = [c for c in range(SIM_CORES) if topo.mates(topo.chip(c), topo.chip(core)) and T.rank_of(c) is None
+            and topo.die(c) == topo.die(core) and topo.may_write(c, core)][0]
     port = [c for c in free if topo.die(c) == topo.die(core) and topo.may_write(c, last)][0]
     return other, port, last
 
@@ -81,26 +81,26 @@ def hand_on(g, core, T, topo):
     n = len(cores)
     for r in range(n):
         other, port, last = helpers_of(r, T, topo)
-        one, two = cores[(r - 1) % n], cores[(r - 2) % n]
         if core == other:
             k = len(near_engines(r, core, T, topo))
-            steps = [(("hx", k), T.xn, "xa", CA, NS, one), (("hy", k), T.xn, "xa", C1, CA, one),
-                     (None, T.xm, "xb", E1, NS, two)]
+            todo = [(("hx", k), T.x1, T.x0, "a1", C1, NS, cores[(r - 1) % n]),
+                    (("hy", k), T.x2, T.x0, "a2", C2, NS, cores[(r - 2) % n]),
+                    (None, T.x3, T.x0, "a3", E1, NS, cores[(r - 3) % n])]
         elif core == port:
-            k = len(near_engines(r, core, T, topo))
-            steps = [(("hx", k), T.xh, "hx", E0, EM, last), (("hy", k), T.xh, "hy", EM, E1, last)]
+            k, to = len(near_engines(r, core, T, topo)), helpers_of(r - 3, T, topo)[2]
+            todo = [(("hx", k), T.x0, T.x0, "hx", E0, EM, to), (("hy", k), T.x0, T.x0, "hy", EM, E1, to)]
         elif core == last:
-            k = len(topo.engines(port, core))
-            steps = [(("hx", k), T.xm, "xb", E0, EM, two), (("hy", k), T.xm, "xb", EM, E1, two)]
+            k = len(topo.engines(helpers_of(r + 3, T, topo)[1], core))
+            todo = [(("hx", k), T.x3, T.x0, "a3", E0, EM, cores[r]), (("hy", k), T.x3, T.x0, "a3", EM, E1, cores[r])]
         else:
             continue
         total = 0
-        for need, win, arrive, lo, hi, to in steps:
+        for need, out, src, arrive, lo, hi, to in todo:
             mine = topo.engines(core, to)
             rid, pid, _ = topo.addr(to)
             if need:
                 g.wait_ge(T.sem[need[0]], need[1])
-            g.remote_dma(win[:, lo:hi], T.xh[:, lo:hi], T.sem[arrive], T.sem.sent, pid, rid, bits(mine))
+            g.remote_dma(out[:, lo:hi], src[:, lo:hi], T.sem[arrive], T.sem.sent, pid, rid, bits(mine))
             total += len(mine)
         g.wait_ge(T.sem.sent, total)
 
@@ -125,14 +125,12 @@ def rank_program(g, core, T, topo):
     def put(qn, key, deps, make):
         work[qn].append((key, deps, make))
 
-    def far_engines(src, dst):
-        return topo.engines(cores[src % n], cores[dst % n])
-
-    arr = {k: (k, len(far_engines(r, q))) for k, r in (("m1", q + 1), ("l1a", q - 1), ("l1b", q - 1))}
-    arr["xa"] = ("xa", len(far_engines(q + 1, q)) + 2 * len(topo.engines(helpers_of(q + 1, T, topo)[0], core)))
-    other2, _, last2 = helpers_of(q + 2, T, topo)
-    arr["xb"] = ("xb", len(far_engines(q + 2, q)) + len(topo.engines(other2, core)) + 2 * len(topo.engines(last2, core)))
-    LD, LD2, LDX = ("ld", 4 * 16), ("ld2", 3 * 16), ("ldx", 8 * 16)
+    other, port, last = helpers_of(q, T, topo)
+    LD, LD2, LDX, LDA = ("ld", 4 * 16), ("ld2", 3 * 16), ("ldx", 8 * 16), ("lda", 8 * 16 * (XA < NS))
+    landed = {0: LDX}
+    for b in (1, 2, 3):
+        senders = [cores[(q + b) % n], helpers_of(q + b, T, topo)[0]] + [last, last] * (b == 3)
+        landed[b] = ("a%d" % b, sum(len(topo.engines(c, core)) for c in senders))
 
     def gathers(b, lo, hi):
         return [o for o in V_ORDER + S_ORDER if o[0] == "g" and o[1] == b and o[2] < hi and o[3] > lo]
@@ -140,139 +138,109 @@ def rank_program(g, core, T, topo):
     def job_of(jobs, b, lo, hi):
         return [j for j, w in jobs.items() if w[0] == b and w[1] < hi and w[2] > lo]
 
-    def load_pa(e, r0):
-        e.dma_start(T.raw[r0:r0 + 8, 0:2], T.pa[:, :]).then_inc(sem.ld, 16)
-
-    def load_de(e, j, name):
-        d = (q + (0, 2, 1, 3)[j]) % n
-        e.dma_start(T.raw[0:64, j:j + 1], T.de[:, 8 * d:8 * d + 8]).then_inc(sem[name], 16)
-
-    def load_x(e, chans):
-        for c in chans:
-            e.dma_start(T.xw[16 * c:16 * c + 16, :], T.x[:, NS * c:NS * (c + 1)]).then_inc(sem.ldx, 16)
-
-    load_de(g.sync, 0, "ld")
-    load_pa(s, 64)
-    load_pa(g.sync, 96)
-    load_pa(s, 72)
-    load_de(g.sync, 3, "ld2")
-    load_de(s, 2, "ld2")
-    load_de(s, 1, "ld2")
-    load_x(g.sync, range(0, 4))
-    load_x(s, range(4, 8))
+    for qn, text in LOADS.items():
+        for what, j in steps(text):
+            if what == "pa":
+                queues[qn].dma_start(T.raw[j:j + 8, 0:2], T.pa[:, :]).then_inc(sem.ld, 16)
+            elif what == "de":
+                d = (q + j) % n
+                queues[qn].dma_start(T.raw[0:64, j:j + 1], T.de[:, 8 * d:8 * d + 8]).then_inc(sem.ld2 if j else sem.ld, 16)
+            else:
+                lo, hi, name = (0, XA, "ldx") if what == "x" else (XA, NS, "lda")
+                queues[qn].dma_start(T.x0[16 * j:16 * j + 16, lo:hi], T.x[:, NS * j + lo:NS * j + hi]).then_inc(sem[name], 16)
 
     sent = [0]
 
-    def send(key, deps, out_ap, in_ap, name, to, eng):
+    def send(out, lo, hi, name, to, eng):
         rid, pid, _ = topo.addr(to)
         sent[0] += len(eng)
-        put("g", key, deps, lambda: g.remote_dma(out_ap, in_ap, sem[name], sem.sent, pid, rid, bits(eng)))
-
-    def far(deps, out_ap, in_ap, name, to):
-        send(None, deps, out_ap, in_ap, name, cores[to % n], far_engines(q, to))
-
-    def near(deps, helper, name, lo, hi):
-        send(None, deps, T.xh[:, lo:hi], T.xw[:, lo:hi], name, helper, near_engines(q, helper, T, topo))
+        put("g", None, [LDA] * (hi > XA) + [LDX] * (lo < XA), lambda: g.remote_dma(out[:, lo:hi], T.x0[:, lo:hi], sem[name], sem.sent, pid, rid, bits(eng)))
 
     def pick(key, deps, view, pat):
         put("g", key, deps, lambda: g.affine_select(view, view, pat, A.is_equal, 0.0, 0, 1))
-
-    def mark_ones(key, deps, view, base):
-        put("g", key, deps, lambda: g.affine_select(view, view, [[-1, view.shape[1]]], A.not_equal, 1.0, base, 1))
 
     pick("maskd", ["mask1"], T.mask[0:64, :], [[-1, 8], [0, 2], [-8, 8]])
     pick("maskq", [], T.mask[64:96, :], [[0, 8], [-8, 2], [-1, 8]])
     pick("maskp", [], T.mask[96:104, :], [[0, 16], [-1, 8]])
     pick("idb", ["idb1", "maskp"], T.idb[:], [[-1, 128]])
-    far([("pqs",)], T.msg1[:, 0:2], T.par[:, 3:5], "m1", q - 1)
-    other, port, _ = helpers_of(q, T, topo)
-    near([LDX], port, "hx", E0, EM)
-    far([], T.xn[:, 0:C1], T.xw[:, 0:C1], "xa", q - 1)
-    near([], other, "hx", CA, NS)
-    near([], port, "hy", EM, E1)
-    near([], other, "hy", E1, CA)
-    far([], T.xm[:, 0:E0], T.xw[:, 0:E0], "xb", q - 2)
-    zeros, sel, fold = T.zb[:, 0:128], T.zb[:, 128:144], T.zb[:, 144:208]
-    put("g", "zb", ["idb"], lambda: g.iota(T.zb[:], [[0, 208]], 0, 0, allow_small_or_imprecise_dtypes=True))
-    for c in range(8):
-        mark_ones(("sel", c), ["zb"] if c == 0 else [("sel", c - 1)], sel, -16 * c)
-    for k in range(2):
-        mark_ones(("fold", k), [("fold", 0)] if k else [("sel", 7)], fold, -64 * k)
-    for k in range(2):
-        far([("ev", k)], T.land1[:, 512 * k:512 * k + 512], T.out1[:, 512 * k:512 * k + 512], "l1" + "ab"[k], q + 1)
+    for way in steps(" ".join(SENDS)):
+        if way[0] == "far":
+            to = cores[(q - way[1]) % n]
+            send(T["x%d" % way[1]], 0, (C1, C2, E0)[way[1] - 1], "a%d" % way[1], to, topo.engines(core, to))
+        elif way[0] == "port":
+            lo, hi, name = ((E0, EM, "hx"), (EM, E1, "hy"))[way[1]]
+            send(T.x0, lo, hi, name, port, near_engines(q, port, T, topo))
+        else:
+            lo, hi, name = ((C1, NS, "hx"), (min(C2, E1), C1, "hy"))[way[1]]
+            send(T.x0, lo, hi, name, other, near_engines(q, other, T, topo))
 
     for key, deps, view, val in (
-            ("mask1", [], T.mask[:], 1.0), ("step0", [], T.step[:], 0.0),
-            ("ini0", [], T.ini[0:64, 0:1], 1.0), ("ini1", [], T.ini[64:96, 0:1], -1.0 / 256),
-            ("ini2", [], T.ini[96:128, 0:1], 3.5), ("idb1", [], T.idb[:], 1.0),
-            ("step1", ["step0"], T.step[64:96, :], 1.0 / 256), ("step2", [], T.step[96:104, 32::32], 1.0 / 512),
-            ("ini3", ["ini2"], T.ini[64:72, 0:1], -2.0 / 256), ("ini4", [], T.ini[96:105, 0:1], -2047.0 / 512),
-            ("qi1", [], T.qi[64:128, 0:1], 1), ("ini5", ["ini4"], T.ini[96:104, 0:1], 0.0)):
+            ("mask1", [], T.mask[:], 1.0), ("ini2", [], T.ini[96:128, 0:1], 3.5),
+            ("ini1", [], T.ini[64:96, 0:1], -1.0 / 256), ("step0", [], T.step[:], 0.0),
+            ("ini4", ["ini2"], T.ini[96:105, 0:1], -2047.0 / 512), ("ini3", ["ini1"], T.ini[64:72, 0:1], -2.0 / 256),
+            ("ini0", [], T.ini[0:64, 0:1], 1.0), ("step1", ["step0"], T.step[64:96, :], 1.0 / 256),
+            ("ini5", ["ini4"], T.ini[96:104, 0:1], 0.0), ("step2", [], T.step[96:104, 32::32], 1.0 / 512),
+            ("idb1", [], T.idb[:], 1.0), ("qi1", [], T.qi[64:128, 0:1], 1)):
         put("v", key, deps, lambda view=view, val=val: v.memset(view, val))
-    put("v", "rhs", ["ini5"], lambda: v.tensor_tensor_scan(T.rhs[:], T.step[:], T.step[:], T.ini[:, 0:1], A.add, A.add))
+    put("v", "rhs", ["step2"], lambda: v.tensor_tensor_scan(T.rhs[:], T.step[:], T.step[:], T.ini[:, 0:1], A.add, A.add))
     for key, deps, view, val in (
-            ("half0", ["step1"], T.big[64:66, 256:384], 1.0 / 32), ("big8", [], T.big[64:65, 0:128], 256 * BIG8),
-            ("half1", ["half0"], T.big[64:65, 256:384], -128.0), ("big1", [], T.big[64:65, 128:256], 256 * BIG1)):
+            ("half0", ["step0"], T.big[64:66, 256:384], 1.0 / 32), ("big8", [], T.big[64:65, 0:128], 256 * BIG8),
+            ("half1", ["half0"], T.big[64:65, 256:384], -128.0), ("big1", [], T.big[64:65, 128:256], 256 * BIG1),
+            ("big3", [], T.big[64:65, 384:512], -256 * BIG1)):
         put("s", key, deps, lambda view=view, val=val: s.activation(
-            view, T.step[64:64 + view.shape[0], 0:128], F.Identity, bias=val, scale=0.0))
+            view, T.step[0:view.shape[0], 0:128], F.Identity, bias=val, scale=0.0))
 
     def delays(lo, hi):
         return v.tensor_scalar(T.par[0:64, lo:hi], T.raw[0:64, lo:hi], float(-CENTER), None, A.add)
 
     put("v", "qa", [LD, "qi1"], lambda: v.tensor_scalar(T.qi[64:80, 0:1], T.raw[64:80, 0:1], 6, None, A.arith_shift_right))
     put("v", "qb", [], lambda: v.tensor_scalar(T.qi[96:104, 0:1], T.raw[96:104, 0:1], 63, None, A.bitwise_and))
-    put("v", "pa", [], lambda: v.tensor_scalar(T.ab[64:80, 0:1], T.raw[64:80, 1:2], 1.0 / 4096, None, A.mult))
     put("v", "pd", [], lambda: delays(0, 1))
     put("v", "pq", ["qb"], lambda: v.tensor_copy(T.par[64:128, 0:1], T.qi[64:128, 0:1]))
-
-    numbers = {0: T.par[0:KROWS, 0:1], 1: T.msg1[0:KROWS, 0:1], 2: T.par[0:KROWS, 2:3], 3: T.par[0:KROWS, 1:2]}
-    accel = {0: T.py[:, 64:65], 1: T.msg1[:, 1:2]}
-    lm_deps = {0: ["pq", "maskp"], 1: [arr["m1"]], 2: [("pqs",)], 3: [("pqs",)]}
-
-    def own_done(k):
-        return pairs(3, OWN[k][1], OWN[k][2]) + [("land", k)]
+    put("v", "pa", [], lambda: v.tensor_scalar(T.ab[64:80, 0:1], T.raw[64:80, 1:2], 1.0 / 4096, None, A.mult))
+    folds = [T.idb, T.f64, T.f32, T.f16]
 
     def elementwise(qn, o):
         kind = o[0]
         if kind == "lm":
             b = o[1]
-            put(qn, o, lm_deps[b], lambda: v.tensor_scalar(
-                T.lm[0:KROWS, 128 * b:128 * b + 128], T.mask[0:KROWS, :], numbers[b], None, A.mult))
+            put(qn, o, [("pqs",), ("pd",)] if b else ["pq", "maskp"], lambda: v.tensor_scalar(
+                T.lm[0:KROWS, 128 * b:128 * b + 128], T.mask[0:KROWS, :], T.par[0:KROWS, b:b + 1], None, A.mult))
         elif kind == "pd":
             put(qn, o, [LD2], lambda: delays(1, 4))
-        elif kind == "acopy":
-            put(qn, o, [("a",)], lambda: v.tensor_copy(T.par[:, 4:5], T.py[:, 64:65]))
+        elif kind == "fold":
+            k, w = o[1], 64 >> o[1]
+            put(qn, o, [("fold", k - 1) if k else "idb"], lambda: v.tensor_tensor(
+                folds[k + 1][:], folds[k][:, 0:w], folds[k][:, w:2 * w], A.add))
         elif kind == "pqs":
             put(qn, o, ["pq"], lambda: v.tensor_scalar(
                 T.par[64:128, 1:4], T.step[64:128, 0:3], 0.0, T.par[64:128, 0:1], A.mult, A.add))
         elif kind == "dg":
-            b = o[1]
-            put(qn, o, ["idb", arr["m1"] if b else ("a",)], lambda: v.tensor_scalar(
-                T.dg[:, 128 * b:128 * b + 128], T.idb[:], accel[b], None, A.mult))
+            put(qn, o, ["idb", ("a",)], lambda: v.tensor_scalar(T.dg[:], T.idb[:], T.py[:, 64:65], None, A.mult))
         elif kind == "sq":
             b, lo, hi, bu = U_JOBS[o[1]][:4]
             put(qn, o, [("u", o[1])], lambda: s.activation(
                 T.sq[:, 512 * b + lo:512 * b + hi], T[bu][:, lo:hi], F.Square, bias=CENTER / 8 - BIG8 / 8, scale=0.125))
         elif kind == "conv":
             b, lo, hi, bt = T_JOBS[o[1]][:4]
-            put(qn, o, [("t", o[1])], lambda: v.tensor_scalar(
-                T.off[:, 512 * b + lo:512 * b + hi], T[bt][:, lo:hi], CENTER - BIG1, None, A.add))
+            how = (BIG1, CENTER - BIG1, A.add, A.add) if o[1] in EARLY else (CENTER - BIG1, None, A.add)
+            put(qn, o, [("t", o[1])], lambda: v.tensor_scalar(T.off[:, 512 * b + lo:512 * b + hi], T[bt][:, lo:hi], *how))
         elif kind == "g":
             b, lo, hi = o[1:]
             out = T["gb%d" % b][:, 16 * lo:16 * hi]
-            src = {2: T.xn, 3: T.xm}.get(b, T.xw)[:, 0:NS].indirect(T.off[:, 512 * b + lo:512 * b + hi])
-            put(qn, o, [("conv", j) for j in job_of(T_JOBS, b, lo, hi)] + [{2: arr["xa"], 3: arr["xb"]}.get(b, LDX)],
+            src = T["x%d" % b][:, 0:NS].indirect(T.off[:, 512 * b + lo:512 * b + hi])
+            put(qn, o, [("conv", j) for j in job_of(T_JOBS, b, lo, hi)] + [landed[b]] + [LDA] * (b == 0),
                 (lambda: v.tensor_copy(out, src)) if qn == "v" else (lambda: s.activation(out, src, F.Copy)))
-        elif kind == "ev":
-            k = o[1]
-            put(qn, o, pairs(1, 4 * k, 4 * k + 4), lambda: s.activation(
-                T.out1[:, 512 * k:512 * k + 512], T["pr%d" % k][:], F.Copy))
         elif kind == "clip":
             bank, lo, hi = OWN[o[1]]
-            put(qn, o, own_done(o[1]), lambda: v.tensor_scalar(
-                T.clip[:, 128 * lo:128 * hi], T[bank][:, 0:128 * (hi - lo)], 255.0, None, A.min))
+            out, src = T.clip[:, 128 * lo:128 * hi], T[bank][:, 0:128 * (hi - lo)]
+            put(qn, o, [r for b in range(n) for r in pairs(b, lo, hi)],
+                (lambda: v.tensor_scalar(out, src, 255.0, -1.0, A.min, A.mult)) if qn == "v" else
+                (lambda: s.activation(out, src, F.Relu, bias=255.0, scale=-1.0)))
         elif kind == "end":
-            put(qn, o, [("sum", k) for k in range(len(OWN))], lambda: v.tensor_copy(T.ysb[:], T.py[:, 0:64]))
+            pulses = sum(2 * (OWN[c[1]][2] - OWN[c[1]][1]) for c in S_ORDER if c[0] == "clip")
+            put(qn, o, [("sum", k) for k in range(len(OWN))],
+                lambda: v.tensor_scalar(T.ysb[:], T.py[:, 0:64], -1.0, 255.0 * pulses, A.mult, A.add))
 
     for qn, order in (("v", V_ORDER), ("s", S_ORDER)):
         for o in order:
@@ -281,79 +249,74 @@ def rank_program(g, core, T, topo):
     def own_bank(m):
         return [k for k, w in enumerate(OWN) if w[1] <= m < w[2]][0]
 
-    last_own = {}
-    for o in P_ORDER:
-        if o[0] == "r" and o[1] == 3:
-            last_own[own_bank(o[2])] = o
-        elif o[0] == "land":
-            last_own[o[1]] = o
+    last_own = {own_bank(o[2]): o for o in P_ORDER if o[0] == "r"}
     sums = [o for o in P_ORDER if o[0] == "sum"]
+    own_banks = [w[0] for w in OWN]
 
     def constant(bank, lo, hi, i, rows, start):
         return p.matmul(T[bank][:, lo:hi], T.big[64:64 + rows, 128 * i:128 * i + 128], T.step[64:64 + rows, lo:hi],
                         start, False)
 
-    def times(bank, b, lo, hi, rows):
-        return p.matmul(T[bank][:, lo:hi], T.lm[0:rows, 128 * b:128 * b + 128], T.rhs[0:rows, lo:hi], False, True)
+    def times(bank, b, lo, hi, rows, stop):
+        return p.matmul(T[bank][:, lo:hi], T.lm[0:rows, 128 * b:128 * b + 128], T.rhs[0:rows, lo:hi], False, stop)
 
     def tensor(o):
         kind = o[0]
-        if kind in ("big8", "half", "u", "t"):
-            b, lo, hi, bu, before = (U_JOBS if kind in ("big8", "u") else T_JOBS)[o[1]]
-            bt, s0 = bu, 128 * (b == 1)
+        if kind in ("big8", "half", "u", "z", "t"):
+            b, lo, hi, bank, before = (U_JOBS if kind in ("big8", "u") else T_JOBS)[o[1]]
+            early = o[1] in EARLY
         if kind == "a":
             put("p", o, ["pa", "maskq"], lambda: p.matmul(T.py[:, 64:65], T.mask[64:80, :], T.ab[64:80, 0:1], True, True))
         elif kind == "big8":
-            put("p", o, ["big8"] + ([("sq", before)] if before else []), lambda: constant(bu, lo, hi, 0, 1, True))
+            put("p", o, ["big8", "step1"] + ([("sq", before)] if before else []), lambda: constant(bank, lo, hi, 0, 1, True))
         elif kind == "half":
-            put("p", o, ["half1"] + ([("conv", before)] if before else []), lambda: constant(bt, lo, hi, 2, 2, True))
+            put("p", o, ["half1", "big1", "step1"] + ([("conv", before)] if before else []),
+                lambda: constant(bank, lo, hi, 1, 1, True) if early else constant(bank, lo, hi, 2, 2, True))
         elif kind == "u":
-            put("p", o, [("lm", b), "rhs"], lambda: times(bu, b, lo, hi, KROWS - 1))
+            put("p", o, [("lm", b), "rhs"], lambda: times(bank, b, lo, hi, KROWS - 1, True))
+        elif kind == "z":
+            def whole():
+                times(bank, b, lo, hi, KROWS, False)
+                constant(bank, lo, hi, 3, 1, False)
+                return constant(bank, lo, hi, 2, 2, False)
+            put("p", o, [("lm", b), "rhs", "big3"], whole)
         elif kind == "t":
             def place():
-                p.matmul(T[bt][:, lo:hi], T.dg[:, s0:s0 + 128], T.sq[:, 512 * b + lo:512 * b + hi], False, False)
-                constant(bt, lo, hi, 1, 1, False)
-                return times(bt, b, lo, hi, KROWS)
-            put("p", o, [("sq", j) for j in job_of(U_JOBS, b, lo, hi)] + [("dg", int(b == 1)), "big1"], place)
+                ins = p.matmul(T[bank][:, lo:hi], T.dg[:], T.sq[:, 512 * b + lo:512 * b + hi], False, early)
+                if not early:
+                    constant(bank, lo, hi, 1, 1, False)
+                    ins = times(bank, b, lo, hi, KROWS, True)
+                return ins
+            put("p", o, [("sq", j) for j in job_of(U_JOBS, b, lo, hi)] + [("dg",)], place)
         elif kind == "open":
             def zero():
                 for bank, lo, hi in OWN:
-                    ins = p.matmul(T[bank][:, 0:128 * (hi - lo)], zeros, T.gb0[:, 0:128 * (hi - lo)], True, False)
+                    ins = p.matmul(T[bank][:, 0:128 * (hi - lo)], T.step[0:1, 0:128], T.step[0:1, 0:128 * (hi - lo)],
+                                   True, False)
                 return ins
-            put("p", o, gathers(0, 0, 32) + ["zb", ("sq", "1"), ("conv", "1"), ("conv", "0c")], zero)
+            put("p", o, [(k, j) for k, jobs in (("sq", U_JOBS), ("conv", T_JOBS)) for j in jobs
+                         if jobs[j][3] in own_banks], zero)
         elif kind == "r":
-            b, m = o[1], o[2]
-            deps = gathers(b, 64 * m, 64 * m + 64) + [("sel", 7)]
-            alone = b == 1
-            if alone:
-                bank, c0, final = "pr%d" % (m // 4), 128 * (m % 4), False
-                deps += [("sq", "2"), ("conv", "2")]
-            else:
-                k = own_bank(m)
-                bank, c0, final = OWN[k][0], 128 * (m - OWN[k][1]), last_own[k] == o
+            b, m = o[1:]
+            k = own_bank(m)
+            bank, c0 = OWN[k][0], 128 * (m - OWN[k][1])
 
             def channels():
                 for t in range(8):
                     ins = p.matmul(T[bank][:, c0 + 16 * t:c0 + 16 * t + 16],
-                                   T["gb%d" % b][:, 1024 * m + t:1024 * m + 1024:8], sel,
-                                   alone, alone or (final and t == 7))
+                                   T["gb%d" % b][:, 1024 * m + t:1024 * m + 1024:8], T.f16[:],
+                                   False, last_own[k] == o and t == 7)
                 return ins
-            put("p", o, deps, channels)
-        elif kind == "land":
-            k = o[1]
-            bank, lo, hi = OWN[k]
-            put("p", o, [arr["l1a" if k == 0 else "l1b"], "idb"], lambda: p.matmul(
-                T[bank][:, 0:128 * (hi - lo)], T.idb[:], T.land1[:, 128 * lo:128 * hi], False, last_own[k] == o))
+            put("p", o, gathers(b, 64 * m, 64 * m + 64) + [("fold", 2)], channels)
         elif kind == "sum":
-            k = o[1]
-            bank, lo, hi = OWN[k]
+            bank, lo, hi = OWN[o[1]]
 
             def pulses():
                 for m in range(lo, hi):
-                    ins = p.matmul(T.py[:, 0:64], T.clip[:, 128 * m:128 * m + 128], fold,
+                    ins = p.matmul(T.py[:, 0:64], T.clip[:, 128 * m:128 * m + 128], T.f64[:],
                                    o == sums[0] and m == lo, o == sums[-1] and m == hi - 1)
                 return ins
-            put("p", o, [("clip", k), ("acopy",), ("fold", 1)], pulses)
+            put("p", o, [("clip", o[1])], pulses)
 
     for o in P_ORDER:
         tensor(o)

from concourse.mybir import AluOpType, ActivationFunctionType

SIM_CORES = 64
NS = 2560
C1, C2, E0, EM, E1 = 1856, 1280, 768, 1280, 1792
XA = C1
SENDS = ["other,0", "far,1", "port,0", "other,1", "far,2", "port,1", "far,3"]
CENTER = 1280
BIG8 = 1.5 * 2.0 ** 26
BIG1 = 1.5 * 2.0 ** 23
KROWS = 106

SCRATCH = {}
for _dt, _bufs in (
        ("int32", dict(raw=4, qi=4)),
        ("float32", dict(ini=4, par=4, dg=128, sq=2048, ysb=64)),
        ("float16", dict(rhs=512, lm=512)),
        ("uint16", dict(off=2048)),
        ("bfloat16", dict(mask=128, idb=128, step=512, big=512, ab=8, f64=64, f32=32, f16=16, x0=NS, x1=NS, x2=NS, x3=NS,
                          gb0=8192, gb1=8192, gb2=8192, gb3=8192, clip=1024))):
    for _k, _w in _bufs.items():
        SCRATCH[_k] = ("sbuf", [128, _w], _dt)
for _k in ("pu", "pt", "pv", "pw", "po0", "po1", "po2", "py"):
    SCRATCH[_k] = ("psum", [128, 512], "float32")
SEMAPHORES = ["sv", "ss", "sp", "sg", "ld", "ld2", "ldx", "lda", "st", "sent", "a1", "a2", "a3", "hx", "hy"]

U_JOBS = {"0a": (0, 0, 128, "pu", None), "0b": (0, 128, 512, "po0", None), "1a": (1, 0, 512, "pv", None),
          "2a": (2, 0, 512, "pu", "0a"), "3a": (3, 0, 512, "pv", "1a")}
T_JOBS = {"0a": (0, 0, 128, "pt", None), "0b": (0, 128, 288, "po1", None), "0c": (0, 288, 512, "po2", None),
          "1a": (1, 0, 512, "pw", None), "2a": (2, 0, 512, "pt", "0a"), "3a": (3, 0, 512, "pw", "1a")}
EARLY = ("0a",)
OWN = [("po0", 0, 4), ("po1", 4, 7), ("po2", 7, 8)]


def pairs(b, lo, hi):
    return [("r", b, m) for m in range(lo, hi)]


def steps(text):
    out = []
    for word in text.split():
        o = tuple(int(x) if x.isdigit() else x for x in word.split(","))
        out += pairs(*o[1:]) if o[0] == "r" else [o]
    return out


V_ORDER = steps("""lm,0 pd pqs dg fold,0 lm,1 fold,1 lm,2 lm,3 conv,0a g,0,64,112 conv,0b conv,0c fold,2 g,0,112,328
    conv,1a conv,2a g,1,256,512 conv,3a g,2,256,512 g,3,0,128 g,3,368,448 g,3,448,484 clip,1 clip,2 end""")
S_ORDER = steps("""sq,0a sq,0b sq,1a g,0,0,64 g,0,328,368 sq,2a sq,3a g,0,368,512 g,1,0,256 g,2,0,256
    g,3,128,320 g,3,320,368 g,3,484,512 clip,0""")
P_ORDER = steps("""big8,0a big8,0b big8,1a half,0a half,0b half,0c a u,0a u,0b z,0a t,0a u,1a t,0b t,0c half,1a
    big8,2a big8,3a u,2a u,3a half,2a t,1a t,2a open half,3a r,0,0,4 t,3a r,0,4,8 r,1,0,8 r,2,0,8 r,3,0,8
    sum,0 sum,1 sum,2""")
LOADS = {"y": "de,0 pa,96 de,3 xa,0 xa,1 xa,2 xa,3 xa,4 xa,5 x,0 x,1 x,2 x,3 x,4 x,5",
         "s": "pa,64 pa,72 de,1 de,2 xa,6 xa,7 x,6 x,7"}


def bits(engines):
    return sum(1 << e for e in engines)


def helpers_of(r, T, topo):
    cores = list(T.cores)
    core = cores[r % len(cores)]
    free = [c for c in topo.cores_of(core) if T.rank_of(c) is None]
    other = [c for c in free if topo.die(c) != topo.die(core)][0]
    last = [c for c in range(SIM_CORES) if topo.mates(topo.chip(c), topo.chip(core)) and T.rank_of(c) is None
            and topo.die(c) == topo.die(core) and topo.may_write(c, core)][0]
    port = [c for c in free if topo.die(c) == topo.die(core) and topo.may_write(c, last)][0]
    return other, port, last


def near_engines(r, helper, T, topo):
    cores = list(T.cores)
    core = cores[r % len(cores)]
    return [e for e in topo.engines(core, helper) if e not in topo.engines(core, cores[(r - 1) % len(cores)])]


def hand_on(g, core, T, topo):
    cores = list(T.cores)
    n = len(cores)
    for r in range(n):
        other, port, last = helpers_of(r, T, topo)
        if core == other:
            k = len(near_engines(r, core, T, topo))
            todo = [(("hx", k), T.x1, T.x0, "a1", C1, NS, cores[(r - 1) % n]),
                    (("hy", k), T.x2, T.x0, "a2", C2, NS, cores[(r - 2) % n]),
                    (None, T.x3, T.x0, "a3", E1, NS, cores[(r - 3) % n])]
        elif core == port:
            k, to = len(near_engines(r, core, T, topo)), helpers_of(r - 3, T, topo)[2]
            todo = [(("hx", k), T.x0, T.x0, "hx", E0, EM, to), (("hy", k), T.x0, T.x0, "hy", EM, E1, to)]
        elif core == last:
            k = len(topo.engines(helpers_of(r + 3, T, topo)[1], core))
            todo = [(("hx", k), T.x3, T.x0, "a3", E0, EM, cores[r]), (("hy", k), T.x3, T.x0, "a3", EM, E1, cores[r])]
        else:
            continue
        total = 0
        for need, out, src, arrive, lo, hi, to in todo:
            mine = topo.engines(core, to)
            rid, pid, _ = topo.addr(to)
            if need:
                g.wait_ge(T.sem[need[0]], need[1])
            g.remote_dma(out[:, lo:hi], src[:, lo:hi], T.sem[arrive], T.sem.sent, pid, rid, bits(mine))
            total += len(mine)
        g.wait_ge(T.sem.sent, total)


def rank_program(g, core, T, topo):
    cores = list(T.cores)
    n = len(cores)
    rank = T.rank_of(core)
    sem = T.sem
    if rank is None:
        hand_on(g, core, T, topo)
        return

    A = AluOpType
    F = ActivationFunctionType
    q = rank
    v, s, p = g.vector, g.scalar, g.tensor
    queues = {"v": v, "s": s, "p": p, "g": g, "y": g.sync}
    own_sem = {"v": "sv", "s": "ss", "p": "sp", "g": "sg"}
    work = {"v": [], "s": [], "p": [], "g": []}

    def put(qn, key, deps, make):
        work[qn].append((key, deps, make))

    other, port, last = helpers_of(q, T, topo)
    LD, LD2, LDX, LDA = ("ld", 4 * 16), ("ld2", 3 * 16), ("ldx", 8 * 16), ("lda", 8 * 16 * (XA < NS))
    landed = {0: LDX}
    for b in (1, 2, 3):
        senders = [cores[(q + b) % n], helpers_of(q + b, T, topo)[0]] + [last, last] * (b == 3)
        landed[b] = ("a%d" % b, sum(len(topo.engines(c, core)) for c in senders))

    def gathers(b, lo, hi):
        return [o for o in V_ORDER + S_ORDER if o[0] == "g" and o[1] == b and o[2] < hi and o[3] > lo]

    def job_of(jobs, b, lo, hi):
        return [j for j, w in jobs.items() if w[0] == b and w[1] < hi and w[2] > lo]

    for qn, text in LOADS.items():
        for what, j in steps(text):
            if what == "pa":
                queues[qn].dma_start(T.raw[j:j + 8, 0:2], T.pa[:, :]).then_inc(sem.ld, 16)
            elif what == "de":
                d = (q + j) % n
                queues[qn].dma_start(T.raw[0:64, j:j + 1], T.de[:, 8 * d:8 * d + 8]).then_inc(sem.ld2 if j else sem.ld, 16)
            else:
                lo, hi, name = (0, XA, "ldx") if what == "x" else (XA, NS, "lda")
                queues[qn].dma_start(T.x0[16 * j:16 * j + 16, lo:hi], T.x[:, NS * j + lo:NS * j + hi]).then_inc(sem[name], 16)

    sent = [0]

    def send(out, lo, hi, name, to, eng):
        rid, pid, _ = topo.addr(to)
        sent[0] += len(eng)
        put("g", None, [LDA] * (hi > XA) + [LDX] * (lo < XA), lambda: g.remote_dma(out[:, lo:hi], T.x0[:, lo:hi], sem[name], sem.sent, pid, rid, bits(eng)))

    def pick(key, deps, view, pat):
        put("g", key, deps, lambda: g.affine_select(view, view, pat, A.is_equal, 0.0, 0, 1))

    pick("maskd", ["mask1"], T.mask[0:64, :], [[-1, 8], [0, 2], [-8, 8]])
    pick("maskq", [], T.mask[64:96, :], [[0, 8], [-8, 2], [-1, 8]])
    pick("maskp", [], T.mask[96:104, :], [[0, 16], [-1, 8]])
    pick("idb", ["idb1", "maskp"], T.idb[:], [[-1, 128]])
    for way in steps(" ".join(SENDS)):
        if way[0] == "far":
            to = cores[(q - way[1]) % n]
            send(T["x%d" % way[1]], 0, (C1, C2, E0)[way[1] - 1], "a%d" % way[1], to, topo.engines(core, to))
        elif way[0] == "port":
            lo, hi, name = ((E0, EM, "hx"), (EM, E1, "hy"))[way[1]]
            send(T.x0, lo, hi, name, port, near_engines(q, port, T, topo))
        else:
            lo, hi, name = ((C1, NS, "hx"), (min(C2, E1), C1, "hy"))[way[1]]
            send(T.x0, lo, hi, name, other, near_engines(q, other, T, topo))

    for key, deps, view, val in (
            ("mask1", [], T.mask[:], 1.0), ("ini2", [], T.ini[96:128, 0:1], 3.5),
            ("ini1", [], T.ini[64:96, 0:1], -1.0 / 256), ("step0", [], T.step[:], 0.0),
            ("ini4", ["ini2"], T.ini[96:105, 0:1], -2047.0 / 512), ("ini3", ["ini1"], T.ini[64:72, 0:1], -2.0 / 256),
            ("ini0", [], T.ini[0:64, 0:1], 1.0), ("step1", ["step0"], T.step[64:96, :], 1.0 / 256),
            ("ini5", ["ini4"], T.ini[96:104, 0:1], 0.0), ("step2", [], T.step[96:104, 32::32], 1.0 / 512),
            ("idb1", [], T.idb[:], 1.0), ("qi1", [], T.qi[64:128, 0:1], 1)):
        put("v", key, deps, lambda view=view, val=val: v.memset(view, val))
    put("v", "rhs", ["step2"], lambda: v.tensor_tensor_scan(T.rhs[:], T.step[:], T.step[:], T.ini[:, 0:1], A.add, A.add))
    for key, deps, view, val in (
            ("half0", ["step0"], T.big[64:66, 256:384], 1.0 / 32), ("big8", [], T.big[64:65, 0:128], 256 * BIG8),
            ("half1", ["half0"], T.big[64:65, 256:384], -128.0), ("big1", [], T.big[64:65, 128:256], 256 * BIG1),
            ("big3", [], T.big[64:65, 384:512], -256 * BIG1)):
        put("s", key, deps, lambda view=view, val=val: s.activation(
            view, T.step[0:view.shape[0], 0:128], F.Identity, bias=val, scale=0.0))

    def delays(lo, hi):
        return v.tensor_scalar(T.par[0:64, lo:hi], T.raw[0:64, lo:hi], float(-CENTER), None, A.add)

    put("v", "qa", [LD, "qi1"], lambda: v.tensor_scalar(T.qi[64:80, 0:1], T.raw[64:80, 0:1], 6, None, A.arith_shift_right))
    put("v", "qb", [], lambda: v.tensor_scalar(T.qi[96:104, 0:1], T.raw[96:104, 0:1], 63, None, A.bitwise_and))
    put("v", "pd", [], lambda: delays(0, 1))
    put("v", "pq", ["qb"], lambda: v.tensor_copy(T.par[64:128, 0:1], T.qi[64:128, 0:1]))
    put("v", "pa", [], lambda: v.tensor_scalar(T.ab[64:80, 0:1], T.raw[64:80, 1:2], 1.0 / 4096, None, A.mult))
    folds = [T.idb, T.f64, T.f32, T.f16]

    def elementwise(qn, o):
        kind = o[0]
        if kind == "lm":
            b = o[1]
            put(qn, o, [("pqs",), ("pd",)] if b else ["pq", "maskp"], lambda: v.tensor_scalar(
                T.lm[0:KROWS, 128 * b:128 * b + 128], T.mask[0:KROWS, :], T.par[0:KROWS, b:b + 1], None, A.mult))
        elif kind == "pd":
            put(qn, o, [LD2], lambda: delays(1, 4))
        elif kind == "fold":
            k, w = o[1], 64 >> o[1]
            put(qn, o, [("fold", k - 1) if k else "idb"], lambda: v.tensor_tensor(
                folds[k + 1][:], folds[k][:, 0:w], folds[k][:, w:2 * w], A.add))
        elif kind == "pqs":
            put(qn, o, ["pq"], lambda: v.tensor_scalar(
                T.par[64:128, 1:4], T.step[64:128, 0:3], 0.0, T.par[64:128, 0:1], A.mult, A.add))
        elif kind == "dg":
            put(qn, o, ["idb", ("a",)], lambda: v.tensor_scalar(T.dg[:], T.idb[:], T.py[:, 64:65], None, A.mult))
        elif kind == "sq":
            b, lo, hi, bu = U_JOBS[o[1]][:4]
            put(qn, o, [("u", o[1])], lambda: s.activation(
                T.sq[:, 512 * b + lo:512 * b + hi], T[bu][:, lo:hi], F.Square, bias=CENTER / 8 - BIG8 / 8, scale=0.125))
        elif kind == "conv":
            b, lo, hi, bt = T_JOBS[o[1]][:4]
            how = (BIG1, CENTER - BIG1, A.add, A.add) if o[1] in EARLY else (CENTER - BIG1, None, A.add)
            put(qn, o, [("t", o[1])], lambda: v.tensor_scalar(T.off[:, 512 * b + lo:512 * b + hi], T[bt][:, lo:hi], *how))
        elif kind == "g":
            b, lo, hi = o[1:]
            out = T["gb%d" % b][:, 16 * lo:16 * hi]
            src = T["x%d" % b][:, 0:NS].indirect(T.off[:, 512 * b + lo:512 * b + hi])
            put(qn, o, [("conv", j) for j in job_of(T_JOBS, b, lo, hi)] + [landed[b]] + [LDA] * (b == 0),
                (lambda: v.tensor_copy(out, src)) if qn == "v" else (lambda: s.activation(out, src, F.Copy)))
        elif kind == "clip":
            bank, lo, hi = OWN[o[1]]
            out, src = T.clip[:, 128 * lo:128 * hi], T[bank][:, 0:128 * (hi - lo)]
            put(qn, o, [r for b in range(n) for r in pairs(b, lo, hi)],
                (lambda: v.tensor_scalar(out, src, 255.0, -1.0, A.min, A.mult)) if qn == "v" else
                (lambda: s.activation(out, src, F.Relu, bias=255.0, scale=-1.0)))
        elif kind == "end":
            pulses = sum(2 * (OWN[c[1]][2] - OWN[c[1]][1]) for c in S_ORDER if c[0] == "clip")
            put(qn, o, [("sum", k) for k in range(len(OWN))],
                lambda: v.tensor_scalar(T.ysb[:], T.py[:, 0:64], -1.0, 255.0 * pulses, A.mult, A.add))

    for qn, order in (("v", V_ORDER), ("s", S_ORDER)):
        for o in order:
            elementwise(qn, o)

    def own_bank(m):
        return [k for k, w in enumerate(OWN) if w[1] <= m < w[2]][0]

    last_own = {own_bank(o[2]): o for o in P_ORDER if o[0] == "r"}
    sums = [o for o in P_ORDER if o[0] == "sum"]
    own_banks = [w[0] for w in OWN]

    def constant(bank, lo, hi, i, rows, start):
        return p.matmul(T[bank][:, lo:hi], T.big[64:64 + rows, 128 * i:128 * i + 128], T.step[64:64 + rows, lo:hi],
                        start, False)

    def times(bank, b, lo, hi, rows, stop):
        return p.matmul(T[bank][:, lo:hi], T.lm[0:rows, 128 * b:128 * b + 128], T.rhs[0:rows, lo:hi], False, stop)

    def tensor(o):
        kind = o[0]
        if kind in ("big8", "half", "u", "z", "t"):
            b, lo, hi, bank, before = (U_JOBS if kind in ("big8", "u") else T_JOBS)[o[1]]
            early = o[1] in EARLY
        if kind == "a":
            put("p", o, ["pa", "maskq"], lambda: p.matmul(T.py[:, 64:65], T.mask[64:80, :], T.ab[64:80, 0:1], True, True))
        elif kind == "big8":
            put("p", o, ["big8", "step1"] + ([("sq", before)] if before else []), lambda: constant(bank, lo, hi, 0, 1, True))
        elif kind == "half":
            put("p", o, ["half1", "big1", "step1"] + ([("conv", before)] if before else []),
                lambda: constant(bank, lo, hi, 1, 1, True) if early else constant(bank, lo, hi, 2, 2, True))
        elif kind == "u":
            put("p", o, [("lm", b), "rhs"], lambda: times(bank, b, lo, hi, KROWS - 1, True))
        elif kind == "z":
            def whole():
                times(bank, b, lo, hi, KROWS, False)
                constant(bank, lo, hi, 3, 1, False)
                return constant(bank, lo, hi, 2, 2, False)
            put("p", o, [("lm", b), "rhs", "big3"], whole)
        elif kind == "t":
            def place():
                ins = p.matmul(T[bank][:, lo:hi], T.dg[:], T.sq[:, 512 * b + lo:512 * b + hi], False, early)
                if not early:
                    constant(bank, lo, hi, 1, 1, False)
                    ins = times(bank, b, lo, hi, KROWS, True)
                return ins
            put("p", o, [("sq", j) for j in job_of(U_JOBS, b, lo, hi)] + [("dg",)], place)
        elif kind == "open":
            def zero():
                for bank, lo, hi in OWN:
                    ins = p.matmul(T[bank][:, 0:128 * (hi - lo)], T.step[0:1, 0:128], T.step[0:1, 0:128 * (hi - lo)],
                                   True, False)
                return ins
            put("p", o, [(k, j) for k, jobs in (("sq", U_JOBS), ("conv", T_JOBS)) for j in jobs
                         if jobs[j][3] in own_banks], zero)
        elif kind == "r":
            b, m = o[1:]
            k = own_bank(m)
            bank, c0 = OWN[k][0], 128 * (m - OWN[k][1])

            def channels():
                for t in range(8):
                    ins = p.matmul(T[bank][:, c0 + 16 * t:c0 + 16 * t + 16],
                                   T["gb%d" % b][:, 1024 * m + t:1024 * m + 1024:8], T.f16[:],
                                   False, last_own[k] == o and t == 7)
                return ins
            put("p", o, gathers(b, 64 * m, 64 * m + 64) + [("fold", 2)], channels)
        elif kind == "sum":
            bank, lo, hi = OWN[o[1]]

            def pulses():
                for m in range(lo, hi):
                    ins = p.matmul(T.py[:, 0:64], T.clip[:, 128 * m:128 * m + 128], T.f64[:],
                                   o == sums[0] and m == lo, o == sums[-1] and m == hi - 1)
                return ins
            put("p", o, [("clip", o[1])], pulses)

    for o in P_ORDER:
        tensor(o)

    done = {}
    for qn, items in work.items():
        for i, key in enumerate([w[0] for w in items if w[0] is not None]):
            done[key] = (own_sem[qn], i + 1)
    seen = {}

    def wait(qn, deps):
        need = {}
        for d in deps:
            name, c = done[d] if d in done else d
            need[name] = max(need.get(name, 0), c)
        for name, c in need.items():
            if seen.get((qn, name), 0) < c:
                queues[qn].wait_ge(sem[name], c)
                seen[(qn, name)] = c

    for qn, items in work.items():
        for key, deps, make in items:
            wait(qn, deps)
            ins = make()
            if key is not None:
                ins.then_inc(sem[own_sem[qn]], 1)

    wait("y", [("end",)])
    g.sync.dma_start(T.y[:, :], T.ysb[:]).then_inc(sem.st, 16)
    g.sync.wait_ge(sem.st, 16)
    wait("g", [("sent", sent[0])] + [(own_sem[qn], sum(w[0] is not None for w in work[qn])) for qn in "gsp"])
